import numpy as np
import ml_dtypes


def mxq(x, axis, fmt="e4m3"):
    dtype, down = {"e4m3": (ml_dtypes.float8_e4m3fn, 7), "e5m2": (ml_dtypes.float8_e5m2, 14)}[fmt]
    v = np.moveaxis(np.asarray(x, np.float32).astype(ml_dtypes.bfloat16).astype(np.float64), axis, -1)
    blocks = v.reshape(v.shape[:-1] + (-1, 32))
    amax = np.abs(blocks).max(-1, keepdims=True)
    byte = np.maximum(np.where(amax > 0, np.frexp(amax)[1] - 1 + 127, 0) - down, 1)
    scale = np.exp2(byte - 127.0)
    codes = (blocks / scale).astype(np.float32).astype(dtype).astype(np.float64)
    return np.moveaxis((codes * scale).reshape(v.shape), -1, axis)


WIDE = False


def mx_kscale(k):
    if not WIDE:
        return np.ones(k)
    levels = np.array([10, -10, 5, -5, 0])
    if k % 512:
        return np.exp2(np.random.permutation(np.resize(levels, k // 32))).repeat(32)
    a = np.empty((k // 512, 16))
    for p in range(k // 512):
        a[p, :8] = np.random.permutation(np.resize(levels, 8))
        for g in range(8):
            far = levels[np.abs(levels - a[p, g]) >= 10]
            a[p, g + 8] = far[np.random.randint(len(far))]
    return np.exp2(a.ravel()).repeat(32)


def f64(x):
    return np.asarray(x).astype(np.float64)


def striped(idx):
    return np.tile(idx.reshape(-1, 16).T, (8, 1)).astype(np.uint16)


def unstriped(offs):
    return offs[:16].T.reshape(-1).astype(np.int64)


E2M1 = np.array([0.0, 0.5, 1.0, 1.5, 2.0, 3.0, 4.0, 6.0, -0.0, -0.5, -1.0, -1.5, -2.0, -3.0, -4.0, -6.0])


def pack_fp4(w):
    k, n = w.shape
    w = f64(np.asarray(w, np.float32).astype(ml_dtypes.bfloat16)).reshape(k // 32, 32, n)
    amax = np.abs(w).max(1)
    mant, ex = np.frexp(amax / 6.0)
    byte = np.clip(np.where(amax > 0, np.where(mant > 0.5, ex, ex - 1) + 127, 1), 1, 254)
    scaled = (w * np.exp2(127.0 - byte)[:, None, :]).reshape(k, n).astype(np.float32)
    c = np.ascontiguousarray(scaled.reshape(k // 512, 128, 4, n).transpose(0, 1, 3, 2)).astype(ml_dtypes.float4_e2m1fn).view(np.uint8) & 0xF
    words = (c[..., 0::2] | (c[..., 1::2] << 4)).reshape(k // 512, 128, 2 * n)
    return np.ascontiguousarray(words), np.ascontiguousarray(byte.astype(np.uint8).reshape(k // 512, 16, n))


def unpack_fp4(words, scales):
    g, _, n = scales.shape
    words = np.ascontiguousarray(words).reshape(g, 128, n, 2)
    nib = np.empty((g, 128, n, 4), np.uint8)
    nib[..., 0::2] = words & 0xF
    nib[..., 1::2] = words >> 4
    vals = E2M1[nib] * np.repeat(np.exp2(scales.astype(np.float64) - 127.0), 8, axis=1)[..., None]
    return vals.transpose(0, 1, 3, 2).reshape(g * 512, n)


K, T, S, N, U = 512, 2048, 1024, 256, 2048
P = 2 ** 7


def setup_inputs():
    n = np.random.standard_normal
    s = mx_kscale(K)[:, None]
    packed_xT = pack_fp4(n((K, T)) * s)
    return {
        "x_words": packed_xT[0],
        "x_scales": packed_xT[1],
        "mem": n((N, U)).astype(np.float32),
        "w1": (n((K, N)) / np.sqrt(K) / s).astype(np.float32),
        "old": np.tile(np.random.uniform(0.5, 0.95, S), (P, 1)).astype(np.float32),
        "new": np.tile(np.random.uniform(0.05, 0.5, S), (P, 1)).astype(np.float32),
        "offs": striped(np.random.permutation(T)[:S]),
        "slot": striped(np.random.permutation(U)[:S]),
    }


def reference(x_words, x_scales, mem, w1, old, new, offs, slot):
    xq = unpack_fp4(x_words, x_scales)[:, unstriped(offs)]
    y = np.tanh(mxq(f64(w1), 0, "e4m3").T @ xq)
    out = f64(mem).copy()
    out[:, unstriped(slot)] = f64(mem)[:, unstriped(slot)] * f64(old)[:1] + y * f64(new)[:1]
    return out

@@ -1,0 +1,132 @@
+from contextlib import ExitStack
+
+import concourse.mybir as mybir
+from concourse.masks import make_identity
+
+K, T, S, N, U = 512, 2048, 1024, 256, 2048
+P = 128
+PACK = 4
+FLOPS = 2 * K * S * N
+BYTES = P * 2 * T + 16 * T + 4 * (2 * N * U + K * N + 2 * S) + 2 * 2 * P * (S // 16)
+
+F32 = mybir.dt.float32
+BF16 = mybir.dt.bfloat16
+I32 = mybir.dt.int32
+U32 = mybir.dt.uint32
+U16 = mybir.dt.uint16
+U8 = mybir.dt.uint8
+FP8X4 = mybir.dt.float8_e4m3fn_x4
+FP4X4 = mybir.dt.float4_e2m1fn_x4
+TANH = mybir.ActivationFunctionType.Tanh
+COPY = mybir.ActivationFunctionType.Copy
+
+BLOCKS = N // P
+TILES = S // P
+HALF = 512
+PIECE = 256
+
+
+def entries(lst, first, count):
+    return lst[:, first // 16 : (first + count) // 16]
+
+
+def tile_picked_ema_tanh_p_kernel(tc, x_words, x_scales, mem, w1, old, new, offs, slot, out):
+    nc = tc.nc
+    with ExitStack() as ctx:
+        keep = ctx.enter_context(tc.tile_pool(name="keep", bufs=1))
+        sums = ctx.enter_context(tc.psum_pool(name="sums", bufs=1))
+        turn = ctx.enter_context(tc.psum_pool(name="turn", bufs=2))
+
+        offs_sb = keep.tile([P, S // 16], U16, name="offs_sb")
+        slot_sb = keep.tile([P, S // 16], U16, name="slot_sb")
+        words = keep.tile([P, T], U16, name="words", align_bytes=64)
+        scales = keep.tile([P, T], U8, name="scales", align_bytes=64)
+        w_raw = keep.tile([P, PACK, N], F32, name="w_raw")
+        window = [keep.tile([P, U], F32, name="window%d" % b) for b in range(BLOCKS)]
+        weight_rows = keep.tile([P, P], F32, name="weight_rows")
+        ident = keep.tile([P, P], F32, name="ident")
+
+        nc.vector.memset(scales[:].bitcast(I32), 0)
+        nc.gpsimd.memset(weight_rows[:], 0.0)
+        make_identity(nc, ident[:])
+        nc.sync.dma_start(offs_sb[:], offs)
+        nc.sync.dma_start(words[:].bitcast(I32), x_words[0].bitcast(I32))
+        for q in range(4):
+            nc.sync.dma_start(scales[32 * q : 32 * q + 4, :].bitcast(I32), x_scales[0, 4 * q : 4 * q + 4, :].bitcast(I32))
+        nc.sync.dma_start(w_raw[:], w1.rearrange("(p t) n -> p t n", t=PACK))
+        nc.sync.dma_start(weight_rows[TILES : 2 * TILES, :], new[0].rearrange("(c j) -> c j", j=P))
+        nc.sync.dma_start(weight_rows[0:TILES, :], old[0].rearrange("(c j) -> c j", j=P))
+        nc.sync.dma_start(slot_sb[:], slot)
+        nc.sync.dma_start(window[0][:], mem[0:P, :])
+        nc.sync.dma_start(window[1][:], mem[P : 2 * P, :])
+
+        w_bf = keep.tile([P, N, PACK], BF16, name="w_bf", tag="w_bf", align_bytes=64)
+        nc.scalar.copy(w_bf[:], w_raw[:].rearrange("p t n -> p n t"))
+
+        weight_ps = turn.tile([P, PIECE], F32, name="updated_ps")
+        nc.tensor.transpose(weight_ps[:, 0:P], weight_rows[:], ident[:])
+        weight_cols = keep.tile([P, 2 * TILES], F32, name="weight_cols")
+        nc.scalar.copy(weight_cols[:], weight_ps[:, 0 : 2 * TILES])
+
+        w_codes = keep.tile([P, N], U32, name="w_codes", align_bytes=64)
+        w_scales = keep.tile([P, N], U8, name="w_scales", align_bytes=64)
+        x_codes = []
+        x_bytes = []
+        for h in range(S // HALF):
+            codes = keep.tile([P, HALF], U16, name="x_codes%d" % h, tag="w_bf" if h else "x_codes", align_bytes=64)
+            sbytes = keep.tile([P, HALF], U8, name="x_bytes%d" % h, align_bytes=64)
+            nc.vector.tensor_copy(codes[:], words[:].indirect(entries(offs_sb, h * HALF, HALF)))
+            nc.vector.tensor_copy(sbytes[:], scales[:].indirect(entries(offs_sb, h * HALF, HALF)))
+            x_codes.append(codes)
+            x_bytes.append(sbytes)
+            if h == 0:
+                nc.vector.quantize_mx(out=w_codes[:].bitcast(FP8X4), scales=w_scales[:], in_=w_bf[:].rearrange("p n t -> p (n t)"))
+
+        picked = {}
+        for b in range(BLOCKS):
+            for h in range(S // HALF):
+                g = keep.tile([P, HALF], F32, name="picked%d_%d" % (b, h))
+                nc.vector.tensor_copy(g[:], window[b][:].indirect(entries(slot_sb, h * HALF, HALF)))
+                picked[b, h] = g
+
+        for b in range(BLOCKS):
+            rows = slice(b * P, (b + 1) * P)
+            new_y = []
+            for h in range(S // HALF):
+                z = sums.tile([P, HALF // P, P], F32, name="z%d_%d" % (b, h))
+                for i in range(HALF // P):
+                    nc.tensor.matmul_mx(
+                        out=z[:, i, :],
+                        lhsT=x_codes[h][:, i * P : (i + 1) * P].bitcast(FP4X4),
+                        lhsT_scale=x_bytes[h][:, i * P : (i + 1) * P],
+                        rhs=w_codes[:, rows].bitcast(FP8X4),
+                        rhs_scale=w_scales[:, rows],
+                        start=True,
+                        stop=True,
+                    )
+                y = keep.tile([P, HALF // P, P], F32, name="y%d_%d" % (b, h))
+                nc.scalar.activation(y[:], z[:], TANH)
+                scaled = keep.tile([P, HALF // P, P], F32, name="new_y%d_%d" % (b, h))
+                for i in range(HALF // P):
+                    col = TILES + h * (HALF // P) + i
+                    nc.scalar.activation(scaled[:, i, :], y[:, i, :], COPY, scale=weight_cols[:, col : col + 1])
+                new_y.append(scaled)
+
+            for pair in range(TILES // 2):
+                h, c = divmod(pair * PIECE, HALF)
+                turned = turn.tile([P, 2, P], F32, name="turned")
+                for i in range(2):
+                    nc.tensor.transpose(turned[:, i, :], picked[b, h][:, c + i * P : c + (i + 1) * P], ident[:])
+                old_mem = keep.tile([P, 2, P], F32, name="old_mem%d_%d" % (b, pair))
+                for i in range(2):
+                    col = 2 * pair + i
+                    nc.scalar.activation(old_mem[:, i, :], turned[:, i, :], COPY, scale=weight_cols[:, col : col + 1])
+                updated_ps = turn.tile([P, PIECE], F32, name="updated_ps")
+                for i in range(2):
+                    cols = slice(i * P, (i + 1) * P)
+                    nc.tensor.matmul(updated_ps[:, cols], new_y[h][:, c // P + i, :], ident[:], start=True, stop=False, is_transpose=True)
+                    nc.tensor.matmul(updated_ps[:, cols], old_mem[:, i, :], ident[:], start=False, stop=True, is_transpose=True)
+                updated = keep.tile([P, PIECE], F32, name="updated%d_%d" % (b, pair))
+                nc.scalar.copy(updated[:], updated_ps[:])
+                nc.vector.tensor_copy(window[b][:].indirect(entries(slot_sb, pair * PIECE, PIECE)), updated[:])
+            nc.sync.dma_start(out[rows, :], window[b][:])

@@ -23,7 +23,6 @@ COPY = mybir.ActivationFunctionType.Copy
 BLOCKS = N // P
 TILES = S // P
 HALF = 512
-PIECE = 256
 
 
 def entries(lst, first, count):
@@ -56,14 +55,14 @@ def tile_picked_ema_tanh_p_kernel(tc, x_words, x_scales, mem, w1, old, new, offs
         nc.sync.dma_start(w_raw[:], w1.rearrange("(p t) n -> p t n", t=PACK))
         nc.sync.dma_start(weight_rows[TILES : 2 * TILES, :], new[0].rearrange("(c j) -> c j", j=P))
         nc.sync.dma_start(weight_rows[0:TILES, :], old[0].rearrange("(c j) -> c j", j=P))
-        nc.sync.dma_start(slot_sb[:], slot)
         nc.sync.dma_start(window[0][:], mem[0:P, :])
+        nc.sync.dma_start(slot_sb[:], slot)
         nc.sync.dma_start(window[1][:], mem[P : 2 * P, :])
 
         w_bf = keep.tile([P, N, PACK], BF16, name="w_bf", tag="w_bf", align_bytes=64)
         nc.scalar.copy(w_bf[:], w_raw[:].rearrange("p t n -> p n t"))
 
-        weight_ps = turn.tile([P, PIECE], F32, name="updated_ps")
+        weight_ps = turn.tile([P, HALF], F32, name="updated_ps")
         nc.tensor.transpose(weight_ps[:, 0:P], weight_rows[:], ident[:])
         weight_cols = keep.tile([P, 2 * TILES], F32, name="weight_cols")
         nc.scalar.copy(weight_cols[:], weight_ps[:, 0 : 2 * TILES])
@@ -93,7 +92,7 @@ def tile_picked_ema_tanh_p_kernel(tc, x_words, x_scales, mem, w1, old, new, offs
             rows = slice(b * P, (b + 1) * P)
             new_y = []
             for h in range(S // HALF):
-                z = sums.tile([P, HALF // P, P], F32, name="z%d_%d" % (b, h))
+                z = sums.tile([P, HALF // P, P], F32, name="z", tag="bank%d" % h if b == 0 else "shared")
                 for i in range(HALF // P):
                     nc.tensor.matmul_mx(
                         out=z[:, i, :],
@@ -112,21 +111,24 @@ def tile_picked_ema_tanh_p_kernel(tc, x_words, x_scales, mem, w1, old, new, offs
                     nc.scalar.activation(scaled[:, i, :], y[:, i, :], COPY, scale=weight_cols[:, col : col + 1])
                 new_y.append(scaled)
 
-            for pair in range(TILES // 2):
-                h, c = divmod(pair * PIECE, HALF)
-                turned = turn.tile([P, 2, P], F32, name="turned")
-                for i in range(2):
-                    nc.tensor.transpose(turned[:, i, :], picked[b, h][:, c + i * P : c + (i + 1) * P], ident[:])
-                old_mem = keep.tile([P, 2, P], F32, name="old_mem%d_%d" % (b, pair))
-                for i in range(2):
-                    col = 2 * pair + i
+            updated = keep.tile([P, S], F32, name="updated%d" % b)
+            for h in range(S // HALF):
+                turned = sums.tile([P, HALF // P, P], F32, name="turned", tag="bank%d" % h if b == 1 else "shared")
+                for i in range(HALF // P):
+                    nc.tensor.transpose(turned[:, i, :], picked[b, h][:, i * P : (i + 1) * P], ident[:])
+                old_mem = keep.tile([P, HALF // P, P], F32, name="old_mem%d_%d" % (b, h))
+                for i in range(HALF // P):
+                    col = h * (HALF // P) + i
                     nc.scalar.activation(old_mem[:, i, :], turned[:, i, :], COPY, scale=weight_cols[:, col : col + 1])
-                updated_ps = turn.tile([P, PIECE], F32, name="updated_ps")
-                for i in range(2):
+                updated_ps = turn.tile([P, HALF], F32, name="updated_ps")
+                for i in range(HALF // P):
                     cols = slice(i * P, (i + 1) * P)
-                    nc.tensor.matmul(updated_ps[:, cols], new_y[h][:, c // P + i, :], ident[:], start=True, stop=False, is_transpose=True)
+                    nc.tensor.matmul(updated_ps[:, cols], new_y[h][:, i, :], ident[:], start=True, stop=False, is_transpose=True)
                     nc.tensor.matmul(updated_ps[:, cols], old_mem[:, i, :], ident[:], start=False, stop=True, is_transpose=True)
-                updated = keep.tile([P, PIECE], F32, name="updated%d_%d" % (b, pair))
-                nc.scalar.copy(updated[:], updated_ps[:])
-                nc.vector.tensor_copy(window[b][:].indirect(entries(slot_sb, pair * PIECE, PIECE)), updated[:])
+                half = slice(h * HALF, (h + 1) * HALF)
+                nc.scalar.copy(updated[:, half], updated_ps[:])
+                if b == 0:
+                    nc.vector.tensor_copy(window[b][:].indirect(entries(slot_sb, h * HALF, HALF)), updated[:, half])
+            if b > 0:
+                nc.vector.tensor_copy(window[b][:].indirect(slot_sb[:]), updated[:])
             nc.sync.dma_start(out[rows, :], window[b][:])

@@ -17,6 +17,8 @@ U16 = mybir.dt.uint16
 U8 = mybir.dt.uint8
 FP8X4 = mybir.dt.float8_e4m3fn_x4
 FP4X4 = mybir.dt.float4_e2m1fn_x4
+MULT = mybir.AluOpType.mult
+ADD = mybir.AluOpType.add
 TANH = mybir.ActivationFunctionType.Tanh
 COPY = mybir.ActivationFunctionType.Copy
 
@@ -33,7 +35,7 @@ def tile_picked_ema_tanh_p_kernel(tc, x_words, x_scales, mem, w1, old, new, offs
     nc = tc.nc
     with ExitStack() as ctx:
         keep = ctx.enter_context(tc.tile_pool(name="keep", bufs=1))
-        sums = ctx.enter_context(tc.psum_pool(name="sums", bufs=1))
+        sums = ctx.enter_context(tc.psum_pool(name="sums", bufs=2))
         turn = ctx.enter_context(tc.psum_pool(name="turn", bufs=2))
 
         offs_sb = keep.tile([P, S // 16], U16, name="offs_sb")
@@ -53,82 +55,59 @@ def tile_picked_ema_tanh_p_kernel(tc, x_words, x_scales, mem, w1, old, new, offs
         for q in range(4):
             nc.sync.dma_start(scales[32 * q : 32 * q + 4, :].bitcast(I32), x_scales[0, 4 * q : 4 * q + 4, :].bitcast(I32))
         nc.sync.dma_start(w_raw[:], w1.rearrange("(p t) n -> p t n", t=PACK))
-        nc.sync.dma_start(weight_rows[TILES : 2 * TILES, :], new[0].rearrange("(c j) -> c j", j=P))
-        nc.sync.dma_start(weight_rows[0:TILES, :], old[0].rearrange("(c j) -> c j", j=P))
-        nc.sync.dma_start(window[0][:], mem[0:P, :])
+        nc.sync.dma_start(weight_rows[0:TILES, :], new[0].rearrange("(c j) -> c j", j=P))
         nc.sync.dma_start(slot_sb[:], slot)
+        nc.sync.dma_start(window[0][:], mem[0:P, :])
+        old_sb = keep.tile([P, S], F32, name="old_sb")
+        nc.sync.dma_start(old_sb[:], old)
         nc.sync.dma_start(window[1][:], mem[P : 2 * P, :])
 
-        w_bf = keep.tile([P, N, PACK], BF16, name="w_bf", tag="w_bf", align_bytes=64)
+        w_bf = keep.tile([P, N, PACK], BF16, name="w_bf", align_bytes=64)
         nc.scalar.copy(w_bf[:], w_raw[:].rearrange("p t n -> p n t"))
 
         weight_ps = turn.tile([P, HALF], F32, name="updated_ps")
         nc.tensor.transpose(weight_ps[:, 0:P], weight_rows[:], ident[:])
-        weight_cols = keep.tile([P, 2 * TILES], F32, name="weight_cols")
-        nc.scalar.copy(weight_cols[:], weight_ps[:, 0 : 2 * TILES])
+        weight_cols = keep.tile([P, TILES], F32, name="weight_cols")
+        nc.scalar.copy(weight_cols[:], weight_ps[:, 0:TILES])
 
         w_codes = keep.tile([P, N], U32, name="w_codes", align_bytes=64)
         w_scales = keep.tile([P, N], U8, name="w_scales", align_bytes=64)
-        x_codes = []
-        x_bytes = []
-        for h in range(S // HALF):
-            codes = keep.tile([P, HALF], U16, name="x_codes%d" % h, tag="w_bf" if h else "x_codes", align_bytes=64)
-            sbytes = keep.tile([P, HALF], U8, name="x_bytes%d" % h, align_bytes=64)
-            nc.vector.tensor_copy(codes[:], words[:].indirect(entries(offs_sb, h * HALF, HALF)))
-            nc.vector.tensor_copy(sbytes[:], scales[:].indirect(entries(offs_sb, h * HALF, HALF)))
-            x_codes.append(codes)
-            x_bytes.append(sbytes)
-            if h == 0:
-                nc.vector.quantize_mx(out=w_codes[:].bitcast(FP8X4), scales=w_scales[:], in_=w_bf[:].rearrange("p n t -> p (n t)"))
+        x_codes = keep.tile([P, S], U16, name="x_codes", align_bytes=64)
+        x_bytes = keep.tile([P, S], U8, name="x_bytes", align_bytes=64)
+        for first in range(0, S, HALF):
+            nc.vector.tensor_copy(x_codes[:, first : first + HALF], words[:].indirect(entries(offs_sb, first, HALF)))
+        nc.vector.tensor_copy(x_bytes[:], scales[:].indirect(offs_sb[:]))
+        nc.vector.quantize_mx(out=w_codes[:].bitcast(FP8X4), scales=w_scales[:], in_=w_bf[:].rearrange("p n t -> p (n t)"))
 
-        picked = {}
+        old_mem = [keep.tile([P, S], F32, name="old_mem%d" % b) for b in range(BLOCKS)]
         for b in range(BLOCKS):
-            for h in range(S // HALF):
-                g = keep.tile([P, HALF], F32, name="picked%d_%d" % (b, h))
-                nc.vector.tensor_copy(g[:], window[b][:].indirect(entries(slot_sb, h * HALF, HALF)))
-                picked[b, h] = g
+            nc.vector.tensor_tensor(old_mem[b][:], window[b][:].indirect(slot_sb[:]), old_sb[:], MULT)
 
         for b in range(BLOCKS):
             rows = slice(b * P, (b + 1) * P)
-            new_y = []
-            for h in range(S // HALF):
-                z = sums.tile([P, HALF // P, P], F32, name="z", tag="bank%d" % h if b == 0 else "shared")
+            new_y = keep.tile([P, S], F32, name="new_y%d" % b)
+            for first in range(0, S, HALF):
+                z = sums.tile([P, HALF // P, P], F32, name="z")
                 for i in range(HALF // P):
+                    cols = slice(first + i * P, first + (i + 1) * P)
                     nc.tensor.matmul_mx(
                         out=z[:, i, :],
-                        lhsT=x_codes[h][:, i * P : (i + 1) * P].bitcast(FP4X4),
-                        lhsT_scale=x_bytes[h][:, i * P : (i + 1) * P],
+                        lhsT=x_codes[:, cols].bitcast(FP4X4),
+                        lhsT_scale=x_bytes[:, cols],
                         rhs=w_codes[:, rows].bitcast(FP8X4),
                         rhs_scale=w_scales[:, rows],
                         start=True,
                         stop=True,
                     )
-                y = keep.tile([P, HALF // P, P], F32, name="y%d_%d" % (b, h))
+                y = keep.tile([P, HALF // P, P], F32, name="y%d_%d" % (b, first))
                 nc.scalar.activation(y[:], z[:], TANH)
-                scaled = keep.tile([P, HALF // P, P], F32, name="new_y%d_%d" % (b, h))
+                scaled = keep.tile([P, HALF // P, P], F32, name="scaled%d_%d" % (b, first))
                 for i in range(HALF // P):
-                    col = TILES + h * (HALF // P) + i
+                    col = first // P + i
                     nc.scalar.activation(scaled[:, i, :], y[:, i, :], COPY, scale=weight_cols[:, col : col + 1])
-                new_y.append(scaled)
-
-            updated = keep.tile([P, S], F32, name="updated%d" % b)
-            for h in range(S // HALF):
-                turned = sums.tile([P, HALF // P, P], F32, name="turned", tag="bank%d" % h if b == 1 else "shared")
+                turned = turn.tile([P, HALF], F32, name="updated_ps")
                 for i in range(HALF // P):
-                    nc.tensor.transpose(turned[:, i, :], picked[b, h][:, i * P : (i + 1) * P], ident[:])
-                old_mem = keep.tile([P, HALF // P, P], F32, name="old_mem%d_%d" % (b, h))
-                for i in range(HALF // P):
-                    col = h * (HALF // P) + i
-                    nc.scalar.activation(old_mem[:, i, :], turned[:, i, :], COPY, scale=weight_cols[:, col : col + 1])
-                updated_ps = turn.tile([P, HALF], F32, name="updated_ps")
-                for i in range(HALF // P):
-                    cols = slice(i * P, (i + 1) * P)
-                    nc.tensor.matmul(updated_ps[:, cols], new_y[h][:, i, :], ident[:], start=True, stop=False, is_transpose=True)
-                    nc.tensor.matmul(updated_ps[:, cols], old_mem[:, i, :], ident[:], start=False, stop=True, is_transpose=True)
-                half = slice(h * HALF, (h + 1) * HALF)
-                nc.scalar.copy(updated[:, half], updated_ps[:])
-                if b == 0:
-                    nc.vector.tensor_copy(window[b][:].indirect(entries(slot_sb, h * HALF, HALF)), updated[:, half])
-            if b > 0:
-                nc.vector.tensor_copy(window[b][:].indirect(slot_sb[:]), updated[:])
+                    nc.tensor.transpose(turned[:, i * P : (i + 1) * P], scaled[:, i, :], ident[:])
+                nc.scalar.copy(new_y[:, first : first + HALF], turned[:])
+            nc.vector.tensor_tensor(window[b][:].indirect(slot_sb[:]), old_mem[b][:], new_y[:], ADD)
             nc.sync.dma_start(out[rows, :], window[b][:])

@@ -56,13 +56,13 @@ def tile_picked_ema_tanh_p_kernel(tc, x_words, x_scales, mem, w1, old, new, offs
             nc.sync.dma_start(scales[32 * q : 32 * q + 4, :].bitcast(I32), x_scales[0, 4 * q : 4 * q + 4, :].bitcast(I32))
         nc.sync.dma_start(w_raw[:], w1.rearrange("(p t) n -> p t n", t=PACK))
         nc.sync.dma_start(weight_rows[0:TILES, :], new[0].rearrange("(c j) -> c j", j=P))
-        nc.sync.dma_start(slot_sb[:], slot)
         nc.sync.dma_start(window[0][:], mem[0:P, :])
+        nc.sync.dma_start(slot_sb[:], slot)
         old_sb = keep.tile([P, S], F32, name="old_sb")
         nc.sync.dma_start(old_sb[:], old)
         nc.sync.dma_start(window[1][:], mem[P : 2 * P, :])
 
-        w_bf = keep.tile([P, N, PACK], BF16, name="w_bf", align_bytes=64)
+        w_bf = keep.tile([P, N, PACK], BF16, name="w_bf", tag="w_bf", align_bytes=64)
         nc.scalar.copy(w_bf[:], w_raw[:].rearrange("p t n -> p n t"))
 
         weight_ps = turn.tile([P, HALF], F32, name="updated_ps")
@@ -73,11 +73,14 @@ def tile_picked_ema_tanh_p_kernel(tc, x_words, x_scales, mem, w1, old, new, offs
         w_codes = keep.tile([P, N], U32, name="w_codes", align_bytes=64)
         w_scales = keep.tile([P, N], U8, name="w_scales", align_bytes=64)
         x_codes = keep.tile([P, S], U16, name="x_codes", align_bytes=64)
-        x_bytes = keep.tile([P, S], U8, name="x_bytes", align_bytes=64)
+        x_bytes = []
         for first in range(0, S, HALF):
             nc.vector.tensor_copy(x_codes[:, first : first + HALF], words[:].indirect(entries(offs_sb, first, HALF)))
-        nc.vector.tensor_copy(x_bytes[:], scales[:].indirect(offs_sb[:]))
-        nc.vector.quantize_mx(out=w_codes[:].bitcast(FP8X4), scales=w_scales[:], in_=w_bf[:].rearrange("p n t -> p (n t)"))
+            sbytes = keep.tile([P, HALF], U8, name="x_bytes", tag="w_bf" if first else "x_bytes", align_bytes=64)
+            nc.vector.tensor_copy(sbytes[:], scales[:].indirect(entries(offs_sb, first, HALF)))
+            x_bytes.append(sbytes)
+            if first == 0:
+                nc.vector.quantize_mx(out=w_codes[:].bitcast(FP8X4), scales=w_scales[:], in_=w_bf[:].rearrange("p n t -> p (n t)"))
 
         old_mem = [keep.tile([P, S], F32, name="old_mem%d" % b) for b in range(BLOCKS)]
         for b in range(BLOCKS):
@@ -93,7 +96,7 @@ def tile_picked_ema_tanh_p_kernel(tc, x_words, x_scales, mem, w1, old, new, offs
                     nc.tensor.matmul_mx(
                         out=z[:, i, :],
                         lhsT=x_codes[:, cols].bitcast(FP4X4),
-                        lhsT_scale=x_bytes[:, cols],
+                        lhsT_scale=x_bytes[first // HALF][:, i * P : (i + 1) * P],
                         rhs=w_codes[:, rows].bitcast(FP8X4),
                         rhs_scale=w_scales[:, rows],
                         start=True,

@@ -25,6 +25,7 @@ COPY = mybir.ActivationFunctionType.Copy
 BLOCKS = N // P
 TILES = S // P
 HALF = 512
+PIECES = ((0, 256), (256, 768))
 
 
 def entries(lst, first, count):
@@ -35,8 +36,7 @@ def tile_picked_ema_tanh_p_kernel(tc, x_words, x_scales, mem, w1, old, new, offs
     nc = tc.nc
     with ExitStack() as ctx:
         keep = ctx.enter_context(tc.tile_pool(name="keep", bufs=1))
-        sums = ctx.enter_context(tc.psum_pool(name="sums", bufs=2))
-        turn = ctx.enter_context(tc.psum_pool(name="turn", bufs=2))
+        psum = ctx.enter_context(tc.psum_pool(name="psum", bufs=1))
 
         offs_sb = keep.tile([P, S // 16], U16, name="offs_sb")
         slot_sb = keep.tile([P, S // 16], U16, name="slot_sb")
@@ -52,20 +52,23 @@ def tile_picked_ema_tanh_p_kernel(tc, x_words, x_scales, mem, w1, old, new, offs
         make_identity(nc, ident[:])
         nc.sync.dma_start(offs_sb[:], offs)
         nc.sync.dma_start(words[:].bitcast(I32), x_words[0].bitcast(I32))
-        for q in range(4):
-            nc.sync.dma_start(scales[32 * q : 32 * q + 4, :].bitcast(I32), x_scales[0, 4 * q : 4 * q + 4, :].bitcast(I32))
         nc.sync.dma_start(w_raw[:], w1.rearrange("(p t) n -> p t n", t=PACK))
+        for r in range(4):
+            nc.sync.dma_start(scales[r:P:32, :].bitcast(I32), x_scales[0, r:16:4, :].bitcast(I32))
         nc.sync.dma_start(weight_rows[0:TILES, :], new[0].rearrange("(c j) -> c j", j=P))
         nc.sync.dma_start(window[0][:], mem[0:P, :])
         nc.sync.dma_start(slot_sb[:], slot)
-        old_sb = keep.tile([P, S], F32, name="old_sb")
-        nc.sync.dma_start(old_sb[:], old)
+        old_sb = []
+        for first, count in PIECES:
+            piece = keep.tile([P, count], F32, name="old_sb", tag="old%d" % first)
+            nc.sync.dma_start(piece[:], old[:, first : first + count])
+            old_sb.append(piece)
         nc.sync.dma_start(window[1][:], mem[P : 2 * P, :])
 
         w_bf = keep.tile([P, N, PACK], BF16, name="w_bf", tag="w_bf", align_bytes=64)
         nc.scalar.copy(w_bf[:], w_raw[:].rearrange("p t n -> p n t"))
 
-        weight_ps = turn.tile([P, HALF], F32, name="updated_ps")
+        weight_ps = psum.tile([P, HALF], F32, name="weight_ps")
         nc.tensor.transpose(weight_ps[:, 0:P], weight_rows[:], ident[:])
         weight_cols = keep.tile([P, TILES], F32, name="weight_cols")
         nc.scalar.copy(weight_cols[:], weight_ps[:, 0:TILES])
@@ -84,13 +87,14 @@ def tile_picked_ema_tanh_p_kernel(tc, x_words, x_scales, mem, w1, old, new, offs
 
         old_mem = [keep.tile([P, S], F32, name="old_mem%d" % b) for b in range(BLOCKS)]
         for b in range(BLOCKS):
-            nc.vector.tensor_tensor(old_mem[b][:], window[b][:].indirect(slot_sb[:]), old_sb[:], MULT)
+            for (first, count), piece in zip(PIECES, old_sb):
+                nc.vector.tensor_tensor(old_mem[b][:, first : first + count], window[b][:].indirect(entries(slot_sb, first, count)), piece[:], MULT)
 
         for b in range(BLOCKS):
             rows = slice(b * P, (b + 1) * P)
-            new_y = keep.tile([P, S], F32, name="new_y%d" % b)
+            new_y = keep.tile([P, S], F32, name="new_y", tag="new_y1" if b else "old0")
             for first in range(0, S, HALF):
-                z = sums.tile([P, HALF // P, P], F32, name="z")
+                z = psum.tile([P, HALF // P, P], F32, name="z", tag="bank%d_%d" % (b, first))
                 for i in range(HALF // P):
                     cols = slice(first + i * P, first + (i + 1) * P)
                     nc.tensor.matmul_mx(
@@ -108,7 +112,7 @@ def tile_picked_ema_tanh_p_kernel(tc, x_words, x_scales, mem, w1, old, new, offs
                 for i in range(HALF // P):
                     col = first // P + i
                     nc.scalar.activation(scaled[:, i, :], y[:, i, :], COPY, scale=weight_cols[:, col : col + 1])
-                turned = turn.tile([P, HALF], F32, name="updated_ps")
+                turned = psum.tile([P, HALF], F32, name="turned", tag="bank%d_%d" % (1 - b, first))
                 for i in range(HALF // P):
                     nc.tensor.transpose(turned[:, i * P : (i + 1) * P], scaled[:, i, :], ident[:])
                 nc.scalar.copy(new_y[:, first : first + HALF], turned[:])

@@ -25,7 +25,7 @@ COPY = mybir.ActivationFunctionType.Copy
 BLOCKS = N // P
 TILES = S // P
 HALF = 512
-PIECES = ((0, 256), (256, 768))
+SCALE_ROW = P - 16
 
 
 def entries(lst, first, count):
@@ -41,66 +41,74 @@ def tile_picked_ema_tanh_p_kernel(tc, x_words, x_scales, mem, w1, old, new, offs
         offs_sb = keep.tile([P, S // 16], U16, name="offs_sb")
         slot_sb = keep.tile([P, S // 16], U16, name="slot_sb")
         words = keep.tile([P, T], U16, name="words", align_bytes=64)
-        scales = keep.tile([P, T], U8, name="scales", align_bytes=64)
-        w_raw = keep.tile([P, PACK, N], F32, name="w_raw")
-        window = [keep.tile([P, U], F32, name="window%d" % b) for b in range(BLOCKS)]
+        scales = keep.tile([P, T], U8, name="scales", tag="window1", align_bytes=64)
+        w_raw = keep.tile([P, PACK, N], F32, name="w_raw", tag="w_raw")
+        window = [keep.tile([P, U], F32, name="window%d" % b, tag="window%d" % b, align_bytes=64) for b in range(BLOCKS)]
+        x_bytes = keep.tile([P, S], U8, name="x_bytes", align_bytes=64)
         weight_rows = keep.tile([P, P], F32, name="weight_rows")
         ident = keep.tile([P, P], F32, name="ident")
 
-        nc.vector.memset(scales[:].bitcast(I32), 0)
+        nc.vector.memset(scales[0:SCALE_ROW, :].bitcast(I32), 0)
         nc.gpsimd.memset(weight_rows[:], 0.0)
         make_identity(nc, ident[:])
+        nc.gpsimd.memset(x_bytes[:].bitcast(I32), 0)
         nc.sync.dma_start(offs_sb[:], offs)
-        nc.sync.dma_start(words[:].bitcast(I32), x_words[0].bitcast(I32))
+        nc.sync.dma_start(scales[SCALE_ROW:P, :].bitcast(I32), x_scales[0].bitcast(I32))
         nc.sync.dma_start(w_raw[:], w1.rearrange("(p t) n -> p t n", t=PACK))
-        for r in range(4):
-            nc.sync.dma_start(scales[r:P:32, :].bitcast(I32), x_scales[0, r:16:4, :].bitcast(I32))
+        nc.sync.dma_start(words[:].bitcast(I32), x_words[0].bitcast(I32))
         nc.sync.dma_start(weight_rows[0:TILES, :], new[0].rearrange("(c j) -> c j", j=P))
+        nc.sync.dma_start(weight_rows[TILES : 2 * TILES, :], old[0].rearrange("(c j) -> c j", j=P))
         nc.sync.dma_start(window[0][:], mem[0:P, :])
         nc.sync.dma_start(slot_sb[:], slot)
-        old_sb = []
-        for first, count in PIECES:
-            piece = keep.tile([P, count], F32, name="old_sb", tag="old%d" % first)
-            nc.sync.dma_start(piece[:], old[:, first : first + count])
-            old_sb.append(piece)
+
+        picked = keep.tile([P, S], U8, name="picked", align_bytes=64)
+        nc.vector.tensor_copy(picked[:], scales[:].indirect(offs_sb[:]))
+        for r in range(4):
+            nc.sync.dma_start(x_bytes[r:P:32, :].bitcast(I32), picked[SCALE_ROW + r : P : 4, :].bitcast(I32))
         nc.sync.dma_start(window[1][:], mem[P : 2 * P, :])
+
+        weight_ps = psum.tile([P, HALF], F32, name="weight_ps")
+        nc.tensor.transpose(weight_ps[:, 0:P], weight_rows[:], ident[:])
+        weight_cols = keep.tile([P, 2 * TILES], F32, name="weight_cols")
+        nc.scalar.copy(weight_cols[:], weight_ps[:, 0 : 2 * TILES])
 
         w_bf = keep.tile([P, N, PACK], BF16, name="w_bf", tag="w_bf", align_bytes=64)
         nc.scalar.copy(w_bf[:], w_raw[:].rearrange("p t n -> p n t"))
 
-        weight_ps = psum.tile([P, HALF], F32, name="weight_ps")
-        nc.tensor.transpose(weight_ps[:, 0:P], weight_rows[:], ident[:])
-        weight_cols = keep.tile([P, TILES], F32, name="weight_cols")
-        nc.scalar.copy(weight_cols[:], weight_ps[:, 0:TILES])
+        old_sb = keep.tile([P, S], F32, name="old_sb", tag="w_raw")
+        for first in range(0, S, HALF):
+            spread = psum.tile([P, HALF], F32, name="spread", tag="bank0_%d" % first)
+            for i in range(HALF // P):
+                col = TILES + first // P + i
+                nc.tensor.transpose(spread[:, i * P : (i + 1) * P], weight_cols[:, col : col + 1].to_broadcast([P, P]), ident[:])
+            nc.scalar.copy(old_sb[:, first : first + HALF], spread[:])
 
         w_codes = keep.tile([P, N], U32, name="w_codes", align_bytes=64)
         w_scales = keep.tile([P, N], U8, name="w_scales", align_bytes=64)
-        x_codes = keep.tile([P, S], U16, name="x_codes", align_bytes=64)
-        x_bytes = []
+        x_codes = []
         for first in range(0, S, HALF):
-            nc.vector.tensor_copy(x_codes[:, first : first + HALF], words[:].indirect(entries(offs_sb, first, HALF)))
-            sbytes = keep.tile([P, HALF], U8, name="x_bytes", tag="w_bf" if first else "x_bytes", align_bytes=64)
-            nc.vector.tensor_copy(sbytes[:], scales[:].indirect(entries(offs_sb, first, HALF)))
-            x_bytes.append(sbytes)
+            codes = keep.tile([P, HALF], U16, name="x_codes", tag="w_bf" if first else "x_codes", align_bytes=64)
+            nc.vector.tensor_copy(codes[:], words[:].indirect(entries(offs_sb, first, HALF)))
+            x_codes.append(codes)
             if first == 0:
                 nc.vector.quantize_mx(out=w_codes[:].bitcast(FP8X4), scales=w_scales[:], in_=w_bf[:].rearrange("p n t -> p (n t)"))
 
         old_mem = [keep.tile([P, S], F32, name="old_mem%d" % b) for b in range(BLOCKS)]
         for b in range(BLOCKS):
-            for (first, count), piece in zip(PIECES, old_sb):
-                nc.vector.tensor_tensor(old_mem[b][:, first : first + count], window[b][:].indirect(entries(slot_sb, first, count)), piece[:], MULT)
+            nc.vector.tensor_tensor(old_mem[b][:], window[b][:].indirect(slot_sb[:]), old_sb[:], MULT)
 
+        z_banks = (("bank0_0", "bank0_512"), ("bank1_512", "bank1_512"))
+        turned_banks = (("bank1_0", "bank1_512"), ("bank0_0", "bank0_512"))
         for b in range(BLOCKS):
             rows = slice(b * P, (b + 1) * P)
-            new_y = keep.tile([P, S], F32, name="new_y", tag="new_y1" if b else "old0")
+            new_y = keep.tile([P, S], F32, name="new_y%d" % b)
             for first in range(0, S, HALF):
-                z = psum.tile([P, HALF // P, P], F32, name="z", tag="bank%d_%d" % (b, first))
+                z = psum.tile([P, HALF // P, P], F32, name="z", tag=z_banks[b][first // HALF])
                 for i in range(HALF // P):
-                    cols = slice(first + i * P, first + (i + 1) * P)
                     nc.tensor.matmul_mx(
                         out=z[:, i, :],
-                        lhsT=x_codes[:, cols].bitcast(FP4X4),
-                        lhsT_scale=x_bytes[first // HALF][:, i * P : (i + 1) * P],
+                        lhsT=x_codes[first // HALF][:, i * P : (i + 1) * P].bitcast(FP4X4),
+                        lhsT_scale=x_bytes[:, first + i * P : first + (i + 1) * P],
                         rhs=w_codes[:, rows].bitcast(FP8X4),
                         rhs_scale=w_scales[:, rows],
                         start=True,
@@ -112,7 +120,7 @@ def tile_picked_ema_tanh_p_kernel(tc, x_words, x_scales, mem, w1, old, new, offs
                 for i in range(HALF // P):
                     col = first // P + i
                     nc.scalar.activation(scaled[:, i, :], y[:, i, :], COPY, scale=weight_cols[:, col : col + 1])
-                turned = psum.tile([P, HALF], F32, name="turned", tag="bank%d_%d" % (1 - b, first))
+                turned = psum.tile([P, HALF], F32, name="turned", tag=turned_banks[b][first // HALF])
                 for i in range(HALF // P):
                     nc.tensor.transpose(turned[:, i * P : (i + 1) * P], scaled[:, i, :], ident[:])
                 nc.scalar.copy(new_y[:, first : first + HALF], turned[:])

@@ -53,11 +53,11 @@ def tile_picked_ema_tanh_p_kernel(tc, x_words, x_scales, mem, w1, old, new, offs
         make_identity(nc, ident[:])
         nc.gpsimd.memset(x_bytes[:].bitcast(I32), 0)
         nc.sync.dma_start(offs_sb[:], offs)
-        nc.sync.dma_start(scales[SCALE_ROW:P, :].bitcast(I32), x_scales[0].bitcast(I32))
+        nc.sync.dma_start(weight_rows[0:TILES, :], new[0].rearrange("(c j) -> c j", j=P))
+        nc.scalar.dma_start(scales[SCALE_ROW:P, :].bitcast(I32), x_scales[0].bitcast(I32))
         nc.sync.dma_start(w_raw[:], w1.rearrange("(p t) n -> p t n", t=PACK))
         nc.sync.dma_start(words[:].bitcast(I32), x_words[0].bitcast(I32))
-        nc.sync.dma_start(weight_rows[0:TILES, :], new[0].rearrange("(c j) -> c j", j=P))
-        nc.sync.dma_start(weight_rows[TILES : 2 * TILES, :], old[0].rearrange("(c j) -> c j", j=P))
+        nc.scalar.dma_start(weight_rows[TILES : 2 * TILES, :], old[0].rearrange("(c j) -> c j", j=P))
         nc.sync.dma_start(window[0][:], mem[0:P, :])
         nc.sync.dma_start(slot_sb[:], slot)
 
@@ -77,7 +77,7 @@ def tile_picked_ema_tanh_p_kernel(tc, x_words, x_scales, mem, w1, old, new, offs
 
         old_sb = keep.tile([P, S], F32, name="old_sb", tag="w_raw")
         for first in range(0, S, HALF):
-            spread = psum.tile([P, HALF], F32, name="spread", tag="bank0_%d" % first)
+            spread = psum.tile([P, HALF], F32, name="spread", tag="product%d" % (first // HALF))
             for i in range(HALF // P):
                 col = TILES + first // P + i
                 nc.tensor.transpose(spread[:, i * P : (i + 1) * P], weight_cols[:, col : col + 1].to_broadcast([P, P]), ident[:])
@@ -97,13 +97,10 @@ def tile_picked_ema_tanh_p_kernel(tc, x_words, x_scales, mem, w1, old, new, offs
         for b in range(BLOCKS):
             nc.vector.tensor_tensor(old_mem[b][:], window[b][:].indirect(slot_sb[:]), old_sb[:], MULT)
 
-        z_banks = (("bank0_0", "bank0_512"), ("bank1_512", "bank1_512"))
-        turned_banks = (("bank1_0", "bank1_512"), ("bank0_0", "bank0_512"))
-        for b in range(BLOCKS):
-            rows = slice(b * P, (b + 1) * P)
-            new_y = keep.tile([P, S], F32, name="new_y%d" % b)
-            for first in range(0, S, HALF):
-                z = psum.tile([P, HALF // P, P], F32, name="z", tag=z_banks[b][first // HALF])
+        for first in range(0, S, HALF):
+            for b in range(BLOCKS):
+                rows = slice(b * P, (b + 1) * P)
+                z = psum.tile([P, HALF // P, P], F32, name="z", tag="product%d" % b)
                 for i in range(HALF // P):
                     nc.tensor.matmul_mx(
                         out=z[:, i, :],
@@ -120,9 +117,11 @@ def tile_picked_ema_tanh_p_kernel(tc, x_words, x_scales, mem, w1, old, new, offs
                 for i in range(HALF // P):
                     col = first // P + i
                     nc.scalar.activation(scaled[:, i, :], y[:, i, :], COPY, scale=weight_cols[:, col : col + 1])
-                turned = psum.tile([P, HALF], F32, name="turned", tag=turned_banks[b][first // HALF])
+                turned = psum.tile([P, HALF], F32, name="turned", tag="turned%d" % b)
                 for i in range(HALF // P):
                     nc.tensor.transpose(turned[:, i * P : (i + 1) * P], scaled[:, i, :], ident[:])
-                nc.scalar.copy(new_y[:, first : first + HALF], turned[:])
-            nc.vector.tensor_tensor(window[b][:].indirect(slot_sb[:]), old_mem[b][:], new_y[:], ADD)
-            nc.sync.dma_start(out[rows, :], window[b][:])
+                new_y = keep.tile([P, HALF], F32, name="new_y%d_%d" % (b, first))
+                nc.scalar.copy(new_y[:], turned[:])
+                nc.vector.tensor_tensor(window[b][:].indirect(entries(slot_sb, first, HALF)), old_mem[b][:, first : first + HALF], new_y[:], ADD)
+        for b in range(BLOCKS):
+            nc.sync.dma_start(out[b * P : (b + 1) * P, :], window[b][:])

@@ -49,15 +49,15 @@ def tile_picked_ema_tanh_p_kernel(tc, x_words, x_scales, mem, w1, old, new, offs
         ident = keep.tile([P, P], F32, name="ident")
 
         nc.vector.memset(scales[0:SCALE_ROW, :].bitcast(I32), 0)
-        nc.gpsimd.memset(weight_rows[:], 0.0)
+        nc.gpsimd.memset(weight_rows[0:SCALE_ROW, :], 0.0)
         make_identity(nc, ident[:])
         nc.gpsimd.memset(x_bytes[:].bitcast(I32), 0)
         nc.sync.dma_start(offs_sb[:], offs)
-        nc.sync.dma_start(weight_rows[0:TILES, :], new[0].rearrange("(c j) -> c j", j=P))
+        nc.sync.dma_start(weight_rows[SCALE_ROW : SCALE_ROW + TILES, :], new[0].rearrange("(c j) -> c j", j=P))
         nc.scalar.dma_start(scales[SCALE_ROW:P, :].bitcast(I32), x_scales[0].bitcast(I32))
         nc.sync.dma_start(w_raw[:], w1.rearrange("(p t) n -> p t n", t=PACK))
         nc.sync.dma_start(words[:].bitcast(I32), x_words[0].bitcast(I32))
-        nc.scalar.dma_start(weight_rows[TILES : 2 * TILES, :], old[0].rearrange("(c j) -> c j", j=P))
+        nc.scalar.dma_start(weight_rows[SCALE_ROW + TILES : P, :], old[0].rearrange("(c j) -> c j", j=P))
         nc.sync.dma_start(window[0][:], mem[0:P, :])
         nc.sync.dma_start(slot_sb[:], slot)
 
@@ -70,7 +70,7 @@ def tile_picked_ema_tanh_p_kernel(tc, x_words, x_scales, mem, w1, old, new, offs
         weight_ps = psum.tile([P, HALF], F32, name="weight_ps")
         nc.tensor.transpose(weight_ps[:, 0:P], weight_rows[:], ident[:])
         weight_cols = keep.tile([P, 2 * TILES], F32, name="weight_cols")
-        nc.scalar.copy(weight_cols[:], weight_ps[:, 0 : 2 * TILES])
+        nc.scalar.copy(weight_cols[:], weight_ps[:, SCALE_ROW:P])
 
         w_bf = keep.tile([P, N, PACK], BF16, name="w_bf", tag="w_bf", align_bytes=64)
         nc.scalar.copy(w_bf[:], w_raw[:].rearrange("p t n -> p n t"))
@@ -97,31 +97,42 @@ def tile_picked_ema_tanh_p_kernel(tc, x_words, x_scales, mem, w1, old, new, offs
         for b in range(BLOCKS):
             nc.vector.tensor_tensor(old_mem[b][:], window[b][:].indirect(slot_sb[:]), old_sb[:], MULT)
 
-        for first in range(0, S, HALF):
-            for b in range(BLOCKS):
-                rows = slice(b * P, (b + 1) * P)
-                z = psum.tile([P, HALF // P, P], F32, name="z", tag="product%d" % b)
-                for i in range(HALF // P):
-                    nc.tensor.matmul_mx(
-                        out=z[:, i, :],
-                        lhsT=x_codes[first // HALF][:, i * P : (i + 1) * P].bitcast(FP4X4),
-                        lhsT_scale=x_bytes[:, first + i * P : first + (i + 1) * P],
-                        rhs=w_codes[:, rows].bitcast(FP8X4),
-                        rhs_scale=w_scales[:, rows],
-                        start=True,
-                        stop=True,
-                    )
-                y = keep.tile([P, HALF // P, P], F32, name="y%d_%d" % (b, first))
-                nc.scalar.activation(y[:], z[:], TANH)
-                scaled = keep.tile([P, HALF // P, P], F32, name="scaled%d_%d" % (b, first))
-                for i in range(HALF // P):
-                    col = first // P + i
-                    nc.scalar.activation(scaled[:, i, :], y[:, i, :], COPY, scale=weight_cols[:, col : col + 1])
-                turned = psum.tile([P, HALF], F32, name="turned", tag="turned%d" % b)
-                for i in range(HALF // P):
-                    nc.tensor.transpose(turned[:, i * P : (i + 1) * P], scaled[:, i, :], ident[:])
-                new_y = keep.tile([P, HALF], F32, name="new_y%d_%d" % (b, first))
-                nc.scalar.copy(new_y[:], turned[:])
-                nc.vector.tensor_tensor(window[b][:].indirect(entries(slot_sb, first, HALF)), old_mem[b][:, first : first + HALF], new_y[:], ADD)
-        for b in range(BLOCKS):
-            nc.sync.dma_start(out[b * P : (b + 1) * P, :], window[b][:])
+        new_y = [keep.tile([P, S], F32, name="new_y%d" % b) for b in range(BLOCKS)]
+
+        def update(b, first):
+            rows = slice(b * P, (b + 1) * P)
+            z = psum.tile([P, HALF // P, P], F32, name="z", tag="product%d" % b)
+            for i in range(HALF // P):
+                nc.tensor.matmul_mx(
+                    out=z[:, i, :],
+                    lhsT=x_codes[first // HALF][:, i * P : (i + 1) * P].bitcast(FP4X4),
+                    lhsT_scale=x_bytes[:, first + i * P : first + (i + 1) * P],
+                    rhs=w_codes[:, rows].bitcast(FP8X4),
+                    rhs_scale=w_scales[:, rows],
+                    start=True,
+                    stop=True,
+                )
+            y = keep.tile([P, HALF // P, P], F32, name="y%d_%d" % (b, first))
+            nc.scalar.activation(y[:], z[:], TANH)
+            scaled = keep.tile([P, HALF // P, P], F32, name="scaled%d_%d" % (b, first))
+            for i in range(HALF // P):
+                col = first // P + i
+                nc.scalar.activation(scaled[:, i, :], y[:, i, :], COPY, scale=weight_cols[:, col : col + 1])
+            turned = psum.tile([P, HALF], F32, name="turned", tag="turned%d" % b)
+            for i in range(HALF // P):
+                nc.tensor.transpose(turned[:, i * P : (i + 1) * P], scaled[:, i, :], ident[:])
+            nc.scalar.copy(new_y[b][:, first : first + HALF], turned[:])
+
+        def scatter(b, first, count):
+            cols = slice(first, first + count)
+            nc.vector.tensor_tensor(window[b][:].indirect(entries(slot_sb, first, count)), old_mem[b][:, cols], new_y[b][:, cols], ADD)
+
+        update(0, 0)
+        scatter(0, 0, HALF)
+        update(1, 0)
+        update(1, HALF)
+        scatter(1, 0, S)
+        nc.sync.dma_start(out[P : 2 * P, :], window[1][:])
+        update(0, HALF)
+        scatter(0, HALF, HALF)
+        nc.sync.dma_start(out[0:P, :], window[0][:])

@@ -25,7 +25,8 @@ COPY = mybir.ActivationFunctionType.Copy
 BLOCKS = N // P
 TILES = S // P
 HALF = 512
-SCALE_ROW = P - 16
+SCALE_ROW = 80
+WEIGHT_ROW = P - 2 * TILES
 
 
 def entries(lst, first, count):
@@ -41,41 +42,42 @@ def tile_picked_ema_tanh_p_kernel(tc, x_words, x_scales, mem, w1, old, new, offs
         offs_sb = keep.tile([P, S // 16], U16, name="offs_sb")
         slot_sb = keep.tile([P, S // 16], U16, name="slot_sb")
         words = keep.tile([P, T], U16, name="words", align_bytes=64)
-        scales = keep.tile([P, T], U8, name="scales", tag="window1", align_bytes=64)
-        w_raw = keep.tile([P, PACK, N], F32, name="w_raw", tag="w_raw")
+        scales = keep.tile([P, T], U8, name="scales", align_bytes=64)
+        w_raw = keep.tile([P, PACK, N], F32, name="w_raw", tag="w_raw", align_bytes=64)
         window = [keep.tile([P, U], F32, name="window%d" % b, tag="window%d" % b, align_bytes=64) for b in range(BLOCKS)]
-        x_bytes = keep.tile([P, S], U8, name="x_bytes", align_bytes=64)
         weight_rows = keep.tile([P, P], F32, name="weight_rows")
         ident = keep.tile([P, P], F32, name="ident")
 
         nc.vector.memset(scales[0:SCALE_ROW, :].bitcast(I32), 0)
-        nc.gpsimd.memset(weight_rows[0:SCALE_ROW, :], 0.0)
+        nc.vector.memset(scales[SCALE_ROW + 16 : P, :].bitcast(I32), 0)
+        nc.gpsimd.memset(weight_rows[0:WEIGHT_ROW, :], 0.0)
         make_identity(nc, ident[:])
-        nc.gpsimd.memset(x_bytes[:].bitcast(I32), 0)
         nc.sync.dma_start(offs_sb[:], offs)
-        nc.sync.dma_start(weight_rows[SCALE_ROW : SCALE_ROW + TILES, :], new[0].rearrange("(c j) -> c j", j=P))
-        nc.scalar.dma_start(scales[SCALE_ROW:P, :].bitcast(I32), x_scales[0].bitcast(I32))
+        nc.sync.dma_start(weight_rows[WEIGHT_ROW : WEIGHT_ROW + TILES, :], new[0].rearrange("(c j) -> c j", j=P))
+        nc.scalar.dma_start(scales[SCALE_ROW : SCALE_ROW + 16, :].bitcast(I32), x_scales[0].bitcast(I32))
         nc.sync.dma_start(w_raw[:], w1.rearrange("(p t) n -> p t n", t=PACK))
         nc.sync.dma_start(words[:].bitcast(I32), x_words[0].bitcast(I32))
-        nc.scalar.dma_start(weight_rows[SCALE_ROW + TILES : P, :], old[0].rearrange("(c j) -> c j", j=P))
+        nc.scalar.dma_start(weight_rows[WEIGHT_ROW + TILES : P, :], old[0].rearrange("(c j) -> c j", j=P))
         nc.sync.dma_start(window[0][:], mem[0:P, :])
         nc.sync.dma_start(slot_sb[:], slot)
 
         picked = keep.tile([P, S], U8, name="picked", align_bytes=64)
         nc.vector.tensor_copy(picked[:], scales[:].indirect(offs_sb[:]))
-        for r in range(4):
-            nc.sync.dma_start(x_bytes[r:P:32, :].bitcast(I32), picked[SCALE_ROW + r : P : 4, :].bitcast(I32))
         nc.sync.dma_start(window[1][:], mem[P : 2 * P, :])
 
         weight_ps = psum.tile([P, HALF], F32, name="weight_ps")
         nc.tensor.transpose(weight_ps[:, 0:P], weight_rows[:], ident[:])
         weight_cols = keep.tile([P, 2 * TILES], F32, name="weight_cols")
-        nc.scalar.copy(weight_cols[:], weight_ps[:, SCALE_ROW:P])
+        nc.scalar.copy(weight_cols[:], weight_ps[:, WEIGHT_ROW:P])
 
         w_bf = keep.tile([P, N, PACK], BF16, name="w_bf", tag="w_bf", align_bytes=64)
         nc.scalar.copy(w_bf[:], w_raw[:].rearrange("p t n -> p n t"))
 
-        old_sb = keep.tile([P, S], F32, name="old_sb", tag="w_raw")
+        x_bytes = keep.tile([P, S], U8, name="x_bytes", tag="w_raw", align_bytes=64)
+        for q in range(4):
+            nc.scalar.dma_start(x_bytes[32 * q : 32 * (q + 1), :].bitcast(I32), picked[SCALE_ROW + 4 * q : SCALE_ROW + 4 * q + 32, :].bitcast(I32))
+
+        old_sb = keep.tile([P, S], F32, name="old_sb")
         for first in range(0, S, HALF):
             spread = psum.tile([P, HALF], F32, name="spread", tag="product%d" % (first // HALF))
             for i in range(HALF // P):

@@ -42,7 +42,7 @@ def tile_picked_ema_tanh_p_kernel(tc, x_words, x_scales, mem, w1, old, new, offs
         offs_sb = keep.tile([P, S // 16], U16, name="offs_sb")
         slot_sb = keep.tile([P, S // 16], U16, name="slot_sb")
         words = keep.tile([P, T], U16, name="words", align_bytes=64)
-        scales = keep.tile([P, T], U8, name="scales", align_bytes=64)
+        scales = keep.tile([P, T], U8, name="scales", tag="window1", align_bytes=64)
         w_raw = keep.tile([P, PACK, N], F32, name="w_raw", tag="w_raw", align_bytes=64)
         window = [keep.tile([P, U], F32, name="window%d" % b, tag="window%d" % b, align_bytes=64) for b in range(BLOCKS)]
         weight_rows = keep.tile([P, P], F32, name="weight_rows")
@@ -55,49 +55,49 @@ def tile_picked_ema_tanh_p_kernel(tc, x_words, x_scales, mem, w1, old, new, offs
         nc.sync.dma_start(offs_sb[:], offs)
         nc.sync.dma_start(weight_rows[WEIGHT_ROW : WEIGHT_ROW + TILES, :], new[0].rearrange("(c j) -> c j", j=P))
         nc.scalar.dma_start(scales[SCALE_ROW : SCALE_ROW + 16, :].bitcast(I32), x_scales[0].bitcast(I32))
-        nc.sync.dma_start(w_raw[:], w1.rearrange("(p t) n -> p t n", t=PACK))
         nc.sync.dma_start(words[:].bitcast(I32), x_words[0].bitcast(I32))
+        nc.sync.dma_start(w_raw[:], w1.rearrange("(p t) n -> p t n", t=PACK))
         nc.scalar.dma_start(weight_rows[WEIGHT_ROW + TILES : P, :], old[0].rearrange("(c j) -> c j", j=P))
         nc.sync.dma_start(window[0][:], mem[0:P, :])
         nc.sync.dma_start(slot_sb[:], slot)
 
         picked = keep.tile([P, S], U8, name="picked", align_bytes=64)
         nc.vector.tensor_copy(picked[:], scales[:].indirect(offs_sb[:]))
+        x_bytes = keep.tile([P, S], U8, name="x_bytes", align_bytes=64)
+        for q in range(4):
+            nc.sync.dma_start(x_bytes[32 * q : 32 * (q + 1), :].bitcast(I32), picked[SCALE_ROW + 4 * q : SCALE_ROW + 4 * q + 32, :].bitcast(I32))
         nc.sync.dma_start(window[1][:], mem[P : 2 * P, :])
 
         weight_ps = psum.tile([P, HALF], F32, name="weight_ps")
         nc.tensor.transpose(weight_ps[:, 0:P], weight_rows[:], ident[:])
-        weight_cols = keep.tile([P, 2 * TILES], F32, name="weight_cols")
-        nc.scalar.copy(weight_cols[:], weight_ps[:, WEIGHT_ROW:P])
-
-        w_bf = keep.tile([P, N, PACK], BF16, name="w_bf", tag="w_bf", align_bytes=64)
-        nc.scalar.copy(w_bf[:], w_raw[:].rearrange("p t n -> p n t"))
-
-        x_bytes = keep.tile([P, S], U8, name="x_bytes", tag="w_raw", align_bytes=64)
-        for q in range(4):
-            nc.scalar.dma_start(x_bytes[32 * q : 32 * (q + 1), :].bitcast(I32), picked[SCALE_ROW + 4 * q : SCALE_ROW + 4 * q + 32, :].bitcast(I32))
+        old_cols = keep.tile([P, TILES], F32, name="old_cols", tag="w_bf", align_bytes=64)
+        nc.scalar.copy(old_cols[:], weight_ps[:, WEIGHT_ROW + TILES : P])
+        new_cols = keep.tile([P, TILES], F32, name="new_cols")
+        nc.scalar.copy(new_cols[:], weight_ps[:, WEIGHT_ROW : WEIGHT_ROW + TILES])
 
         old_sb = keep.tile([P, S], F32, name="old_sb")
         for first in range(0, S, HALF):
             spread = psum.tile([P, HALF], F32, name="spread", tag="product%d" % (first // HALF))
             for i in range(HALF // P):
-                col = TILES + first // P + i
-                nc.tensor.transpose(spread[:, i * P : (i + 1) * P], weight_cols[:, col : col + 1].to_broadcast([P, P]), ident[:])
+                col = first // P + i
+                nc.tensor.transpose(spread[:, i * P : (i + 1) * P], old_cols[:, col : col + 1].to_broadcast([P, P]), ident[:])
             nc.scalar.copy(old_sb[:, first : first + HALF], spread[:])
+
+        w_bf = keep.tile([P, N, PACK], BF16, name="w_bf", tag="w_bf", align_bytes=64)
+        nc.scalar.copy(w_bf[:], w_raw[:].rearrange("p t n -> p n t"))
 
         w_codes = keep.tile([P, N], U32, name="w_codes", align_bytes=64)
         w_scales = keep.tile([P, N], U8, name="w_scales", align_bytes=64)
         x_codes = []
         for first in range(0, S, HALF):
-            codes = keep.tile([P, HALF], U16, name="x_codes", tag="w_bf" if first else "x_codes", align_bytes=64)
+            codes = keep.tile([P, HALF], U16, name="x_codes", tag="x_codes%d" % first, align_bytes=64)
             nc.vector.tensor_copy(codes[:], words[:].indirect(entries(offs_sb, first, HALF)))
             x_codes.append(codes)
-            if first == 0:
-                nc.vector.quantize_mx(out=w_codes[:].bitcast(FP8X4), scales=w_scales[:], in_=w_bf[:].rearrange("p n t -> p (n t)"))
+        nc.vector.quantize_mx(out=w_codes[:].bitcast(FP8X4), scales=w_scales[:], in_=w_bf[:].rearrange("p n t -> p (n t)"))
 
-        old_mem = [keep.tile([P, S], F32, name="old_mem%d" % b) for b in range(BLOCKS)]
+        old_mem = keep.tile([P, BLOCKS, S], F32, name="old_mem", tag="w_bf", align_bytes=64)
         for b in range(BLOCKS):
-            nc.vector.tensor_tensor(old_mem[b][:], window[b][:].indirect(slot_sb[:]), old_sb[:], MULT)
+            nc.vector.tensor_tensor(old_mem[:, b, :], window[b][:].indirect(slot_sb[:]), old_sb[:], MULT)
 
         new_y = [keep.tile([P, S], F32, name="new_y%d" % b) for b in range(BLOCKS)]
 
@@ -119,7 +119,7 @@ def tile_picked_ema_tanh_p_kernel(tc, x_words, x_scales, mem, w1, old, new, offs
             scaled = keep.tile([P, HALF // P, P], F32, name="scaled%d_%d" % (b, first))
             for i in range(HALF // P):
                 col = first // P + i
-                nc.scalar.activation(scaled[:, i, :], y[:, i, :], COPY, scale=weight_cols[:, col : col + 1])
+                nc.scalar.activation(scaled[:, i, :], y[:, i, :], COPY, scale=new_cols[:, col : col + 1])
             turned = psum.tile([P, HALF], F32, name="turned", tag="turned%d" % b)
             for i in range(HALF // P):
                 nc.tensor.transpose(turned[:, i * P : (i + 1) * P], scaled[:, i, :], ident[:])
@@ -127,7 +127,7 @@ def tile_picked_ema_tanh_p_kernel(tc, x_words, x_scales, mem, w1, old, new, offs
 
         def scatter(b, first, count):
             cols = slice(first, first + count)
-            nc.vector.tensor_tensor(window[b][:].indirect(entries(slot_sb, first, count)), old_mem[b][:, cols], new_y[b][:, cols], ADD)
+            nc.vector.tensor_tensor(window[b][:].indirect(entries(slot_sb, first, count)), old_mem[:, b, cols], new_y[b][:, cols], ADD)
 
         update(0, 0)
         scatter(0, 0, HALF)

@@ -22,11 +22,12 @@ ADD = mybir.AluOpType.add
 TANH = mybir.ActivationFunctionType.Tanh
 COPY = mybir.ActivationFunctionType.Copy
 
-BLOCKS = N // P
+ROW_GROUPS = N // P
 TILES = S // P
 HALF = 512
-SCALE_ROW = 80
-WEIGHT_ROW = P - 2 * TILES
+SCALE_ROWS = K // 32
+QUADRANT = 32
+TOP = P - 16
 
 
 def entries(lst, first, count):
@@ -44,36 +45,38 @@ def tile_picked_ema_tanh_p_kernel(tc, x_words, x_scales, mem, w1, old, new, offs
         words = keep.tile([P, T], U16, name="words", align_bytes=64)
         scales = keep.tile([P, T], U8, name="scales", tag="window1", align_bytes=64)
         w_raw = keep.tile([P, PACK, N], F32, name="w_raw", tag="w_raw", align_bytes=64)
-        window = [keep.tile([P, U], F32, name="window%d" % b, tag="window%d" % b, align_bytes=64) for b in range(BLOCKS)]
+        window = [keep.tile([P, U], F32, name="window%d" % b, tag="window%d" % b, align_bytes=64) for b in range(ROW_GROUPS)]
+        x_bytes = keep.tile([P, S], U8, name="x_bytes", align_bytes=64)
         weight_rows = keep.tile([P, P], F32, name="weight_rows")
         ident = keep.tile([P, P], F32, name="ident")
 
-        nc.vector.memset(scales[0:SCALE_ROW, :].bitcast(I32), 0)
-        nc.vector.memset(scales[SCALE_ROW + 16 : P, :].bitcast(I32), 0)
-        nc.gpsimd.memset(weight_rows[0:WEIGHT_ROW, :], 0.0)
+        nc.vector.memset(scales[0:TOP, :].bitcast(I32), 0)
+        nc.gpsimd.memset(weight_rows[0:TOP, :], 0.0)
         make_identity(nc, ident[:])
+        nc.gpsimd.memset(x_bytes[:].bitcast(I32), 0)
+
         nc.sync.dma_start(offs_sb[:], offs)
-        nc.sync.dma_start(weight_rows[WEIGHT_ROW : WEIGHT_ROW + TILES, :], new[0].rearrange("(c j) -> c j", j=P))
-        nc.scalar.dma_start(scales[SCALE_ROW : SCALE_ROW + 16, :].bitcast(I32), x_scales[0].bitcast(I32))
+        nc.sync.dma_start(weight_rows[TOP : TOP + TILES, :], new[0].rearrange("(c j) -> c j", j=P))
+        nc.scalar.dma_start(scales[TOP:P, :].bitcast(I32), x_scales[0].bitcast(I32))
         nc.sync.dma_start(words[:].bitcast(I32), x_words[0].bitcast(I32))
         nc.sync.dma_start(w_raw[:], w1.rearrange("(p t) n -> p t n", t=PACK))
-        nc.scalar.dma_start(weight_rows[WEIGHT_ROW + TILES : P, :], old[0].rearrange("(c j) -> c j", j=P))
+        nc.scalar.dma_start(weight_rows[TOP + TILES : P, :], old[0].rearrange("(c j) -> c j", j=P))
         nc.sync.dma_start(window[0][:], mem[0:P, :])
         nc.sync.dma_start(slot_sb[:], slot)
 
         picked = keep.tile([P, S], U8, name="picked", align_bytes=64)
         nc.vector.tensor_copy(picked[:], scales[:].indirect(offs_sb[:]))
-        x_bytes = keep.tile([P, S], U8, name="x_bytes", align_bytes=64)
-        for q in range(4):
-            nc.sync.dma_start(x_bytes[32 * q : 32 * (q + 1), :].bitcast(I32), picked[SCALE_ROW + 4 * q : SCALE_ROW + 4 * q + 32, :].bitcast(I32))
+        step = SCALE_ROWS // (P // QUADRANT)
+        for r in range(step):
+            nc.sync.dma_start(x_bytes[r:P:QUADRANT, :].bitcast(I32), picked[TOP + r : P : step, :].bitcast(I32))
         nc.sync.dma_start(window[1][:], mem[P : 2 * P, :])
 
         weight_ps = psum.tile([P, HALF], F32, name="weight_ps")
         nc.tensor.transpose(weight_ps[:, 0:P], weight_rows[:], ident[:])
         old_cols = keep.tile([P, TILES], F32, name="old_cols", tag="w_bf", align_bytes=64)
-        nc.scalar.copy(old_cols[:], weight_ps[:, WEIGHT_ROW + TILES : P])
+        nc.scalar.copy(old_cols[:], weight_ps[:, TOP + TILES : P])
         new_cols = keep.tile([P, TILES], F32, name="new_cols")
-        nc.scalar.copy(new_cols[:], weight_ps[:, WEIGHT_ROW : WEIGHT_ROW + TILES])
+        nc.scalar.copy(new_cols[:], weight_ps[:, TOP : TOP + TILES])
 
         old_sb = keep.tile([P, S], F32, name="old_sb")
         for first in range(0, S, HALF):
@@ -95,13 +98,13 @@ def tile_picked_ema_tanh_p_kernel(tc, x_words, x_scales, mem, w1, old, new, offs
             x_codes.append(codes)
         nc.vector.quantize_mx(out=w_codes[:].bitcast(FP8X4), scales=w_scales[:], in_=w_bf[:].rearrange("p n t -> p (n t)"))
 
-        old_mem = keep.tile([P, BLOCKS, S], F32, name="old_mem", tag="w_bf", align_bytes=64)
-        for b in range(BLOCKS):
+        old_mem = keep.tile([P, ROW_GROUPS, S], F32, name="old_mem", tag="w_raw", align_bytes=64)
+        for b in range(ROW_GROUPS):
             nc.vector.tensor_tensor(old_mem[:, b, :], window[b][:].indirect(slot_sb[:]), old_sb[:], MULT)
 
-        new_y = [keep.tile([P, S], F32, name="new_y%d" % b) for b in range(BLOCKS)]
+        new_y = [keep.tile([P, S], F32, name="new_y%d" % b) for b in range(ROW_GROUPS)]
 
-        def update(b, first):
+        def project(b, first):
             rows = slice(b * P, (b + 1) * P)
             z = psum.tile([P, HALF // P, P], F32, name="z", tag="product%d" % b)
             for i in range(HALF // P):
@@ -129,12 +132,12 @@ def tile_picked_ema_tanh_p_kernel(tc, x_words, x_scales, mem, w1, old, new, offs
             cols = slice(first, first + count)
             nc.vector.tensor_tensor(window[b][:].indirect(entries(slot_sb, first, count)), old_mem[:, b, cols], new_y[b][:, cols], ADD)
 
-        update(0, 0)
+        project(0, 0)
         scatter(0, 0, HALF)
-        update(1, 0)
-        update(1, HALF)
+        project(1, 0)
+        project(1, HALF)
         scatter(1, 0, S)
         nc.sync.dma_start(out[P : 2 * P, :], window[1][:])
-        update(0, HALF)
+        project(0, HALF)
         scatter(0, HALF, HALF)
         nc.sync.dma_start(out[0:P, :], window[0][:])

@@ -42,7 +42,7 @@ def tile_picked_ema_tanh_p_kernel(tc, x_words, x_scales, mem, w1, old, new, offs
 
         offs_sb = keep.tile([P, S // 16], U16, name="offs_sb")
         slot_sb = keep.tile([P, S // 16], U16, name="slot_sb")
-        words = keep.tile([P, T], U16, name="words", align_bytes=64)
+        words = keep.tile([P, 2 * T], U16, name="words", align_bytes=64)
         scales = keep.tile([P, T], U8, name="scales", tag="window1", align_bytes=64)
         w_raw = keep.tile([P, PACK, N], F32, name="w_raw", tag="w_raw", align_bytes=64)
         window = [keep.tile([P, U], F32, name="window%d" % b, tag="window%d" % b, align_bytes=64) for b in range(ROW_GROUPS)]
@@ -51,6 +51,7 @@ def tile_picked_ema_tanh_p_kernel(tc, x_words, x_scales, mem, w1, old, new, offs
         ident = keep.tile([P, P], F32, name="ident")
 
         nc.vector.memset(scales[0:TOP, :].bitcast(I32), 0)
+        nc.vector.memset(words[:].bitcast(I32)[:, T // 2 : T], 0)
         nc.gpsimd.memset(weight_rows[0:TOP, :], 0.0)
         make_identity(nc, ident[:])
         nc.gpsimd.memset(x_bytes[:].bitcast(I32), 0)
@@ -58,7 +59,7 @@ def tile_picked_ema_tanh_p_kernel(tc, x_words, x_scales, mem, w1, old, new, offs
         nc.sync.dma_start(offs_sb[:], offs)
         nc.sync.dma_start(weight_rows[TOP : TOP + TILES, :], new[0].rearrange("(c j) -> c j", j=P))
         nc.scalar.dma_start(scales[TOP:P, :].bitcast(I32), x_scales[0].bitcast(I32))
-        nc.sync.dma_start(words[:].bitcast(I32), x_words[0].bitcast(I32))
+        nc.sync.dma_start(words[:].bitcast(I32)[:, 0 : T // 2], x_words[0].bitcast(I32))
         nc.sync.dma_start(w_raw[:], w1.rearrange("(p t) n -> p t n", t=PACK))
         nc.scalar.dma_start(weight_rows[TOP + TILES : P, :], old[0].rearrange("(c j) -> c j", j=P))
         nc.sync.dma_start(window[0][:], mem[0:P, :])
@@ -91,11 +92,8 @@ def tile_picked_ema_tanh_p_kernel(tc, x_words, x_scales, mem, w1, old, new, offs
 
         w_codes = keep.tile([P, N], U32, name="w_codes", align_bytes=64)
         w_scales = keep.tile([P, N], U8, name="w_scales", align_bytes=64)
-        x_codes = []
-        for first in range(0, S, HALF):
-            codes = keep.tile([P, HALF], U16, name="x_codes", tag="x_codes%d" % first, align_bytes=64)
-            nc.vector.tensor_copy(codes[:], words[:].indirect(entries(offs_sb, first, HALF)))
-            x_codes.append(codes)
+        x_codes = keep.tile([P, S], U16, name="x_codes", align_bytes=64)
+        nc.vector.tensor_copy(x_codes[:], words[:].indirect(offs_sb[:]))
         nc.vector.quantize_mx(out=w_codes[:].bitcast(FP8X4), scales=w_scales[:], in_=w_bf[:].rearrange("p n t -> p (n t)"))
 
         old_mem = keep.tile([P, ROW_GROUPS, S], F32, name="old_mem", tag="w_raw", align_bytes=64)
@@ -110,7 +108,7 @@ def tile_picked_ema_tanh_p_kernel(tc, x_words, x_scales, mem, w1, old, new, offs
             for i in range(HALF // P):
                 nc.tensor.matmul_mx(
                     out=z[:, i, :],
-                    lhsT=x_codes[first // HALF][:, i * P : (i + 1) * P].bitcast(FP4X4),
+                    lhsT=x_codes[:, first + i * P : first + (i + 1) * P].bitcast(FP4X4),
                     lhsT_scale=x_bytes[:, first + i * P : first + (i + 1) * P],
                     rhs=w_codes[:, rows].bitcast(FP8X4),
                     rhs_scale=w_scales[:, rows],

@@ -28,6 +28,7 @@ HALF = 512
 SCALE_ROWS = K // 32
 QUADRANT = 32
 TOP = P - 16
+STEP = 256
 
 
 def entries(lst, first, count):
@@ -102,40 +103,39 @@ def tile_picked_ema_tanh_p_kernel(tc, x_words, x_scales, mem, w1, old, new, offs
 
         new_y = [keep.tile([P, S], F32, name="new_y%d" % b) for b in range(ROW_GROUPS)]
 
-        def project(b, first):
+        def project(b, first, count, bank, turn):
             rows = slice(b * P, (b + 1) * P)
-            z = psum.tile([P, HALF // P, P], F32, name="z", tag="product%d" % b)
-            for i in range(HALF // P):
+            z = psum.tile([P, HALF], F32, name="z", tag="product%d" % bank)
+            for at in range(first, first + count, P):
                 nc.tensor.matmul_mx(
-                    out=z[:, i, :],
-                    lhsT=x_codes[:, first + i * P : first + (i + 1) * P].bitcast(FP4X4),
-                    lhsT_scale=x_bytes[:, first + i * P : first + (i + 1) * P],
+                    out=z[:, at - first : at - first + P],
+                    lhsT=x_codes[:, at : at + P].bitcast(FP4X4),
+                    lhsT_scale=x_bytes[:, at : at + P],
                     rhs=w_codes[:, rows].bitcast(FP8X4),
                     rhs_scale=w_scales[:, rows],
                     start=True,
                     stop=True,
                 )
-            y = keep.tile([P, HALF // P, P], F32, name="y%d_%d" % (b, first))
-            nc.scalar.activation(y[:], z[:], TANH)
-            scaled = keep.tile([P, HALF // P, P], F32, name="scaled%d_%d" % (b, first))
-            for i in range(HALF // P):
+            y = keep.tile([P, count], F32, name="y", tag="y%d_%d" % (b, first))
+            nc.scalar.activation(y[:], z[:, 0:count], TANH)
+            scaled = keep.tile([P, count], F32, name="scaled%d_%d" % (b, first))
+            for i in range(count // P):
                 col = first // P + i
-                nc.scalar.activation(scaled[:, i, :], y[:, i, :], COPY, scale=new_cols[:, col : col + 1])
-            turned = psum.tile([P, HALF], F32, name="turned", tag="turned%d" % b)
-            for i in range(HALF // P):
-                nc.tensor.transpose(turned[:, i * P : (i + 1) * P], scaled[:, i, :], ident[:])
-            nc.scalar.copy(new_y[b][:, first : first + HALF], turned[:])
+                nc.scalar.activation(scaled[:, i * P : (i + 1) * P], y[:, i * P : (i + 1) * P], COPY, scale=new_cols[:, col : col + 1])
+            turned = psum.tile([P, HALF], F32, name="turned", tag="turned%d" % turn)
+            for i in range(count // P):
+                nc.tensor.transpose(turned[:, i * P : (i + 1) * P], scaled[:, i * P : (i + 1) * P], ident[:])
+            nc.scalar.copy(new_y[b][:, first : first + count], turned[:, 0:count])
 
         def scatter(b, first, count):
             cols = slice(first, first + count)
             nc.vector.tensor_tensor(window[b][:].indirect(entries(slot_sb, first, count)), old_mem[:, b, cols], new_y[b][:, cols], ADD)
 
-        project(0, 0)
-        scatter(0, 0, HALF)
-        project(1, 0)
-        project(1, HALF)
-        scatter(1, 0, S)
-        nc.sync.dma_start(out[P : 2 * P, :], window[1][:])
-        project(0, HALF)
-        scatter(0, HALF, HALF)
-        nc.sync.dma_start(out[0:P, :], window[0][:])
+        done = 0
+        for b, first, count in ((0, 0, HALF), (1, 0, S), (0, HALF, HALF)):
+            for at in range(first, first + count, STEP):
+                project(b, at, STEP, done % 2, done % 4)
+                done = done + 1
+            scatter(b, first, count)
+            if first + count == S:
+                nc.sync.dma_start(out[b * P : (b + 1) * P, :], window[b][:])

@@ -75,21 +75,25 @@ def tile_picked_ema_tanh_p_kernel(tc, x_words, x_scales, mem, w1, old, new, offs
 
         weight_ps = psum.tile([P, HALF], F32, name="weight_ps")
         nc.tensor.transpose(weight_ps[:, 0:P], weight_rows[:], ident[:])
-        old_cols = keep.tile([P, TILES], F32, name="old_cols", tag="w_bf", align_bytes=64)
-        nc.scalar.copy(old_cols[:], weight_ps[:, TOP + TILES : P])
+        old_cols = [
+            keep.tile([P, HALF // P], F32, name="old_first", tag="w_bf", align_bytes=64),
+            keep.tile([P, HALF // P], F32, name="old_second"),
+        ]
+        for h in range(2):
+            at = TOP + TILES + h * HALF // P
+            nc.scalar.copy(old_cols[h][:], weight_ps[:, at : at + HALF // P])
         new_cols = keep.tile([P, TILES], F32, name="new_cols")
         nc.scalar.copy(new_cols[:], weight_ps[:, TOP : TOP + TILES])
 
         old_sb = keep.tile([P, S], F32, name="old_sb")
-        for first in range(0, S, HALF):
-            spread = psum.tile([P, HALF], F32, name="spread", tag="product%d" % (first // HALF))
+        spread = [psum.tile([P, HALF], F32, name="spread", tag="product%d" % h) for h in range(2)]
+        for h in range(2):
             for i in range(HALF // P):
-                col = first // P + i
-                nc.tensor.transpose(spread[:, i * P : (i + 1) * P], old_cols[:, col : col + 1].to_broadcast([P, P]), ident[:])
-            nc.scalar.copy(old_sb[:, first : first + HALF], spread[:])
-
+                nc.tensor.transpose(spread[h][:, i * P : (i + 1) * P], old_cols[h][:, i : i + 1].to_broadcast([P, P]), ident[:])
+        nc.scalar.copy(old_sb[:, 0:HALF], spread[0][:])
         w_bf = keep.tile([P, N, PACK], BF16, name="w_bf", tag="w_bf", align_bytes=64)
-        nc.scalar.copy(w_bf[:], w_raw[:].rearrange("p t n -> p n t"))
+        nc.scalar.copy(w_bf[:].rearrange("p (c i) t -> p c t i", i=4), w_raw[:].rearrange("p t (c i) -> p c t i", i=4))
+        nc.scalar.copy(old_sb[:, HALF:S], spread[1][:])
 
         w_codes = keep.tile([P, N], U32, name="w_codes", align_bytes=64)
         w_scales = keep.tile([P, N], U8, name="w_scales", align_bytes=64)

@@ -136,7 +136,7 @@ def tile_picked_ema_tanh_p_kernel(tc, x_words, x_scales, mem, w1, old, new, offs
             nc.vector.tensor_tensor(window[b][:].indirect(entries(slot_sb, first, count)), old_mem[:, b, cols], new_y[b][:, cols], ADD)
 
         done = 0
-        for b, first, count in ((0, 0, HALF), (1, 0, S), (0, HALF, HALF)):
+        for b, first, count in ((0, 0, HALF), (1, 0, STEP), (0, HALF, HALF), (1, STEP, S - STEP)):
             for at in range(first, first + count, STEP):
                 project(b, at, STEP, done % 2, done % 4)
                 done = done + 1

@@ -29,6 +29,8 @@ SCALE_ROWS = K // 32
 QUADRANT = 32
 TOP = P - 16
 STEP = 256
+PIECE = 256
+RUN = 4
 
 
 def entries(lst, first, count):
@@ -92,8 +94,12 @@ def tile_picked_ema_tanh_p_kernel(tc, x_words, x_scales, mem, w1, old, new, offs
                 nc.tensor.transpose(spread[h][:, i * P : (i + 1) * P], old_cols[h][:, i : i + 1].to_broadcast([P, P]), ident[:])
         nc.scalar.copy(old_sb[:, 0:HALF], spread[0][:])
         w_bf = keep.tile([P, N, PACK], BF16, name="w_bf", tag="w_bf", align_bytes=64)
-        nc.scalar.copy(w_bf[:].rearrange("p (c i) t -> p c t i", i=4), w_raw[:].rearrange("p t (c i) -> p c t i", i=4))
+        nc.scalar.copy(w_bf[:].rearrange("p (c i) t -> p c t i", i=RUN), w_raw[:].rearrange("p t (c i) -> p c t i", i=RUN))
         nc.scalar.copy(old_sb[:, HALF:S], spread[1][:])
+        new_ps = [psum.tile([P, HALF], F32, name="new_ps%d" % h) for h in range(2)]
+        for c in range(TILES):
+            at = c * P % HALF
+            nc.tensor.transpose(new_ps[c * P // HALF][:, at : at + P], new_cols[:, c : c + 1].to_broadcast([P, P]), ident[:])
 
         w_codes = keep.tile([P, N], U32, name="w_codes", align_bytes=64)
         w_scales = keep.tile([P, N], U8, name="w_scales", align_bytes=64)
@@ -102,44 +108,58 @@ def tile_picked_ema_tanh_p_kernel(tc, x_words, x_scales, mem, w1, old, new, offs
         nc.vector.quantize_mx(out=w_codes[:].bitcast(FP8X4), scales=w_scales[:], in_=w_bf[:].rearrange("p n t -> p (n t)"))
 
         old_mem = keep.tile([P, ROW_GROUPS, S], F32, name="old_mem", tag="w_raw", align_bytes=64)
-        for b in range(ROW_GROUPS):
-            nc.vector.tensor_tensor(old_mem[:, b, :], window[b][:].indirect(slot_sb[:]), old_sb[:], MULT)
+        nc.vector.tensor_tensor(old_mem[:, 0, :], window[0][:].indirect(slot_sb[:]), old_sb[:], MULT)
 
-        new_y = [keep.tile([P, S], F32, name="new_y%d" % b) for b in range(ROW_GROUPS)]
-
-        def project(b, first, count, bank, turn):
-            rows = slice(b * P, (b + 1) * P)
-            z = psum.tile([P, HALF], F32, name="z", tag="product%d" % bank)
-            for at in range(first, first + count, P):
+        turned = [psum.tile([P, HALF], F32, name="turned%d" % h) for h in range(2)]
+        for first in range(0, S, STEP):
+            z = psum.tile([P, HALF], F32, name="z", tag="product%d" % (first // STEP % 2))
+            for at in range(first, first + STEP, P):
                 nc.tensor.matmul_mx(
                     out=z[:, at - first : at - first + P],
                     lhsT=x_codes[:, at : at + P].bitcast(FP4X4),
                     lhsT_scale=x_bytes[:, at : at + P],
-                    rhs=w_codes[:, rows].bitcast(FP8X4),
-                    rhs_scale=w_scales[:, rows],
+                    rhs=w_codes[:, 0:P].bitcast(FP8X4),
+                    rhs_scale=w_scales[:, 0:P],
                     start=True,
                     stop=True,
                 )
-            y = keep.tile([P, count], F32, name="y", tag="y%d_%d" % (b, first))
-            nc.scalar.activation(y[:], z[:, 0:count], TANH)
-            scaled = keep.tile([P, count], F32, name="scaled%d_%d" % (b, first))
-            for i in range(count // P):
+            y = keep.tile([P, STEP], F32, name="y%d" % first)
+            nc.scalar.activation(y[:], z[:, 0:STEP], TANH)
+            scaled = keep.tile([P, STEP], F32, name="scaled%d" % first)
+            for i in range(STEP // P):
                 col = first // P + i
                 nc.scalar.activation(scaled[:, i * P : (i + 1) * P], y[:, i * P : (i + 1) * P], COPY, scale=new_cols[:, col : col + 1])
-            turned = psum.tile([P, HALF], F32, name="turned", tag="turned%d" % turn)
-            for i in range(count // P):
-                nc.tensor.transpose(turned[:, i * P : (i + 1) * P], scaled[:, i * P : (i + 1) * P], ident[:])
-            nc.scalar.copy(new_y[b][:, first : first + count], turned[:, 0:count])
+            for i in range(STEP // P):
+                at = first % HALF + i * P
+                nc.tensor.transpose(turned[first // HALF][:, at : at + P], scaled[:, i * P : (i + 1) * P], ident[:])
 
-        def scatter(b, first, count):
-            cols = slice(first, first + count)
-            nc.vector.tensor_tensor(window[b][:].indirect(entries(slot_sb, first, count)), old_mem[:, b, cols], new_y[b][:, cols], ADD)
+        y_rows = keep.tile([P, S], F32, name="y_rows")
+        for h in range(2):
+            cols = slice(h * HALF, (h + 1) * HALF)
+            z = psum.tile([P, HALF], F32, name="z", tag="product%d" % h)
+            nc.tensor.matmul_mx(
+                out=z[:],
+                lhsT=w_codes[:, P:N].bitcast(FP8X4),
+                lhsT_scale=w_scales[:, P:N],
+                rhs=x_codes[:, cols].bitcast(FP4X4),
+                rhs_scale=x_bytes[:, cols],
+                start=True,
+                stop=True,
+            )
+            nc.scalar.activation(y_rows[:, cols], z[:], TANH)
 
-        done = 0
-        for b, first, count in ((0, 0, HALF), (1, 0, STEP), (0, HALF, HALF), (1, STEP, S - STEP)):
-            for at in range(first, first + count, STEP):
-                project(b, at, STEP, done % 2, done % 4)
-                done = done + 1
-            scatter(b, first, count)
-            if first + count == S:
-                nc.sync.dma_start(out[b * P : (b + 1) * P, :], window[b][:])
+        summed = [keep.tile([P, HALF], F32, name="summed%d" % h) for h in range(2)]
+        new_y = keep.tile([P, S], F32, name="new_y")
+        nc.vector.tensor_tensor(summed[0][:], turned[0][:], old_mem[:, 0, 0:HALF], ADD)
+        nc.vector.tensor_tensor(old_mem[:, 1, :], window[1][:].indirect(slot_sb[:]), old_sb[:], MULT)
+        for h in range(2):
+            cols = slice(h * HALF, (h + 1) * HALF)
+            nc.vector.tensor_tensor(new_y[:, cols], new_ps[h][:], y_rows[:, cols], MULT)
+        nc.vector.tensor_tensor(summed[1][:], turned[1][:], old_mem[:, 0, HALF:S], ADD)
+
+        for first in range(0, S, PIECE):
+            at = first % HALF
+            nc.scalar.activation(window[0][:].indirect(entries(slot_sb, first, PIECE)), summed[first // HALF][:, at : at + PIECE], COPY)
+        nc.sync.dma_start(out[0:P, :], window[0][:])
+        nc.vector.tensor_tensor(window[1][:].indirect(slot_sb[:]), old_mem[:, 1, :], new_y[:], ADD)
+        nc.sync.dma_start(out[P:N, :], window[1][:])

@@ -28,8 +28,7 @@ HALF = 512
 SCALE_ROWS = K // 32
 QUADRANT = 32
 TOP = P - 16
-STEP = 256
-PIECE = 256
+PIECE = 384
 RUN = 4
 
 
@@ -75,7 +74,7 @@ def tile_picked_ema_tanh_p_kernel(tc, x_words, x_scales, mem, w1, old, new, offs
             nc.sync.dma_start(x_bytes[r:P:QUADRANT, :].bitcast(I32), picked[TOP + r : P : step, :].bitcast(I32))
         nc.sync.dma_start(window[1][:], mem[P : 2 * P, :])
 
-        weight_ps = psum.tile([P, HALF], F32, name="weight_ps")
+        weight_ps = psum.tile([P, HALF], F32, name="weight_ps", tag="product0")
         nc.tensor.transpose(weight_ps[:, 0:P], weight_rows[:], ident[:])
         old_cols = [
             keep.tile([P, HALF // P], F32, name="old_first", tag="w_bf", align_bytes=64),
@@ -88,7 +87,7 @@ def tile_picked_ema_tanh_p_kernel(tc, x_words, x_scales, mem, w1, old, new, offs
         nc.scalar.copy(new_cols[:], weight_ps[:, TOP : TOP + TILES])
 
         old_sb = keep.tile([P, S], F32, name="old_sb")
-        spread = [psum.tile([P, HALF], F32, name="spread", tag="product%d" % h) for h in range(2)]
+        spread = [psum.tile([P, HALF], F32, name="spread", tag="product%d" % (1 + h)) for h in range(2)]
         for h in range(2):
             for i in range(HALF // P):
                 nc.tensor.transpose(spread[h][:, i * P : (i + 1) * P], old_cols[h][:, i : i + 1].to_broadcast([P, P]), ident[:])
@@ -96,7 +95,7 @@ def tile_picked_ema_tanh_p_kernel(tc, x_words, x_scales, mem, w1, old, new, offs
         w_bf = keep.tile([P, N, PACK], BF16, name="w_bf", tag="w_bf", align_bytes=64)
         nc.scalar.copy(w_bf[:].rearrange("p (c i) t -> p c t i", i=RUN), w_raw[:].rearrange("p t (c i) -> p c t i", i=RUN))
         nc.scalar.copy(old_sb[:, HALF:S], spread[1][:])
-        new_ps = [psum.tile([P, HALF], F32, name="new_ps%d" % h) for h in range(2)]
+        new_ps = [psum.tile([P, HALF], F32, name="new_ps", tag="new%d" % h) for h in range(2)]
         for c in range(TILES):
             at = c * P % HALF
             nc.tensor.transpose(new_ps[c * P // HALF][:, at : at + P], new_cols[:, c : c + 1].to_broadcast([P, P]), ident[:])
@@ -107,13 +106,50 @@ def tile_picked_ema_tanh_p_kernel(tc, x_words, x_scales, mem, w1, old, new, offs
         nc.vector.tensor_copy(x_codes[:], words[:].indirect(offs_sb[:]))
         nc.vector.quantize_mx(out=w_codes[:].bitcast(FP8X4), scales=w_scales[:], in_=w_bf[:].rearrange("p n t -> p (n t)"))
 
-        old_mem = keep.tile([P, ROW_GROUPS, S], F32, name="old_mem", tag="w_raw", align_bytes=64)
-        nc.vector.tensor_tensor(old_mem[:, 0, :], window[0][:].indirect(slot_sb[:]), old_sb[:], MULT)
+        gathered = keep.tile([P, S + HALF], F32, name="gathered", tag="w_raw", align_bytes=64)
+        old_mem0 = gathered[:, 0:S]
+        mem_late = gathered[:, S : S + HALF]
+        nc.vector.tensor_tensor(old_mem0[:, 0:HALF], window[0][:].indirect(entries(slot_sb, 0, HALF)), old_sb[:, 0:HALF], MULT)
+        nc.scalar.activation(mem_late, window[0][:].indirect(entries(slot_sb, HALF, HALF)), COPY)
+        nc.vector.tensor_tensor(old_mem0[:, HALF:S], mem_late, old_sb[:, HALF:S], MULT)
 
-        turned = [psum.tile([P, HALF], F32, name="turned%d" % h) for h in range(2)]
-        for first in range(0, S, STEP):
-            z = psum.tile([P, HALF], F32, name="z", tag="product%d" % (first // STEP % 2))
-            for at in range(first, first + STEP, P):
+        def project_rows(z, y, b, first, count):
+            cols = slice(first, first + count)
+            rows = slice(b * P, (b + 1) * P)
+            nc.tensor.matmul_mx(
+                out=z[:, 0:count],
+                lhsT=w_codes[:, rows].bitcast(FP8X4),
+                lhsT_scale=w_scales[:, rows],
+                rhs=x_codes[:, cols].bitcast(FP4X4),
+                rhs_scale=x_bytes[:, cols],
+                start=True,
+                stop=True,
+            )
+            nc.scalar.activation(y[:], z[:, 0:count], TANH)
+
+        short = S % PIECE
+        pieces = [(0, short)] + [(first, PIECE) for first in range(short, S, PIECE)]
+        summed = keep.tile([P, S], F32, name="summed")
+        new_y = keep.tile([P, S], F32, name="new_y")
+
+        z_short = psum.tile([P, HALF], F32, name="z_short", tag="product0")
+        y_short = keep.tile([P, short], F32, name="y_short")
+        project_rows(z_short, y_short, 0, 0, short)
+        new_y_short = keep.tile([P, short], F32, name="new_y_short")
+        nc.vector.tensor_tensor(new_y_short[:], new_ps[0][:, 0:short], y_short[:], MULT)
+
+        z_first = psum.tile([P, HALF], F32, name="z_first")
+        y_first = keep.tile([P, HALF], F32, name="y_first", tag="y_first")
+        project_rows(z_first, y_first, 1, 0, HALF)
+        nc.vector.tensor_tensor(new_y[:, 0:HALF], new_ps[0][:], y_first[:], MULT)
+        nc.vector.tensor_tensor(summed[:, 0:short], new_y_short[:], old_mem0[:, 0:short], ADD)
+        old_mem1 = keep.tile([P, S], F32, name="old_mem1", tag="y_first")
+        nc.vector.tensor_tensor(old_mem1[:], window[1][:].indirect(slot_sb[:]), old_sb[:], MULT)
+
+        turned = {}
+        for n, (first, count) in list(enumerate(pieces))[1:]:
+            z = psum.tile([P, HALF], F32, name="z", tag="product%d" % n)
+            for at in range(first, first + count, P):
                 nc.tensor.matmul_mx(
                     out=z[:, at - first : at - first + P],
                     lhsT=x_codes[:, at : at + P].bitcast(FP4X4),
@@ -123,43 +159,39 @@ def tile_picked_ema_tanh_p_kernel(tc, x_words, x_scales, mem, w1, old, new, offs
                     start=True,
                     stop=True,
                 )
-            y = keep.tile([P, STEP], F32, name="y%d" % first)
-            nc.scalar.activation(y[:], z[:, 0:STEP], TANH)
-            scaled = keep.tile([P, STEP], F32, name="scaled%d" % first)
-            for i in range(STEP // P):
+            y = keep.tile([P, count], F32, name="y%d" % n)
+            nc.scalar.activation(y[:], z[:, 0:count], TANH)
+            scaled = keep.tile([P, count], F32, name="scaled%d" % n)
+            for i in range(count // P):
                 col = first // P + i
                 nc.scalar.activation(scaled[:, i * P : (i + 1) * P], y[:, i * P : (i + 1) * P], COPY, scale=new_cols[:, col : col + 1])
-            for i in range(STEP // P):
-                at = first % HALF + i * P
-                nc.tensor.transpose(turned[first // HALF][:, at : at + P], scaled[:, i * P : (i + 1) * P], ident[:])
+            turned[n] = psum.tile([P, HALF], F32, name="turned%d" % n)
+            for i in range(count // P):
+                nc.tensor.transpose(turned[n][:, i * P : (i + 1) * P], scaled[:, i * P : (i + 1) * P], ident[:])
 
-        y_rows = keep.tile([P, S], F32, name="y_rows")
-        for h in range(2):
-            cols = slice(h * HALF, (h + 1) * HALF)
-            z = psum.tile([P, HALF], F32, name="z", tag="product%d" % h)
-            nc.tensor.matmul_mx(
-                out=z[:],
-                lhsT=w_codes[:, P:N].bitcast(FP8X4),
-                lhsT_scale=w_scales[:, P:N],
-                rhs=x_codes[:, cols].bitcast(FP4X4),
-                rhs_scale=x_bytes[:, cols],
-                start=True,
-                stop=True,
-            )
-            nc.scalar.activation(y_rows[:, cols], z[:], TANH)
+        def add(n):
+            first, count = pieces[n]
+            cols = slice(first, first + count)
+            nc.vector.tensor_tensor(summed[:, cols], turned[n][:, 0:count], old_mem0[:, cols], ADD)
 
-        summed = [keep.tile([P, HALF], F32, name="summed%d" % h) for h in range(2)]
-        new_y = keep.tile([P, S], F32, name="new_y")
-        nc.vector.tensor_tensor(summed[0][:], turned[0][:], old_mem[:, 0, 0:HALF], ADD)
-        nc.vector.tensor_tensor(old_mem[:, 1, :], window[1][:].indirect(slot_sb[:]), old_sb[:], MULT)
-        for h in range(2):
-            cols = slice(h * HALF, (h + 1) * HALF)
-            nc.vector.tensor_tensor(new_y[:, cols], new_ps[h][:], y_rows[:, cols], MULT)
-        nc.vector.tensor_tensor(summed[1][:], turned[1][:], old_mem[:, 0, HALF:S], ADD)
+        def scatter(n):
+            first, count = pieces[n]
+            nc.scalar.activation(window[0][:].indirect(entries(slot_sb, first, count)), summed[:, first : first + count], COPY)
 
-        for first in range(0, S, PIECE):
-            at = first % HALF
-            nc.scalar.activation(window[0][:].indirect(entries(slot_sb, first, PIECE)), summed[first // HALF][:, at : at + PIECE], COPY)
+        def put(first, count):
+            cols = slice(first, first + count)
+            nc.vector.tensor_tensor(window[1][:].indirect(entries(slot_sb, first, count)), old_mem1[:, cols], new_y[:, cols], ADD)
+
+        scatter(0)
+        z_second = psum.tile([P, HALF], F32, name="z_second", tag="new0")
+        y_second = keep.tile([P, HALF], F32, name="y_second")
+        project_rows(z_second, y_second, 1, HALF, HALF)
+        add(1)
+        put(0, short)
+        nc.vector.tensor_tensor(new_y[:, HALF:S], new_ps[1][:], y_second[:], MULT)
+        add(2)
+        put(short, S - short)
+        scatter(1)
+        scatter(2)
         nc.sync.dma_start(out[0:P, :], window[0][:])
-        nc.vector.tensor_tensor(window[1][:].indirect(slot_sb[:]), old_mem[:, 1, :], new_y[:], ADD)
         nc.sync.dma_start(out[P:N, :], window[1][:])

@@ -127,71 +127,67 @@ def tile_picked_ema_tanh_p_kernel(tc, x_words, x_scales, mem, w1, old, new, offs
             )
             nc.scalar.activation(y[:], z[:, 0:count], TANH)
 
-        short = S % PIECE
-        pieces = [(0, short)] + [(first, PIECE) for first in range(short, S, PIECE)]
         summed = keep.tile([P, S], F32, name="summed")
         new_y = keep.tile([P, S], F32, name="new_y")
 
-        z_short = psum.tile([P, HALF], F32, name="z_short", tag="product0")
-        y_short = keep.tile([P, short], F32, name="y_short")
-        project_rows(z_short, y_short, 0, 0, short)
-        new_y_short = keep.tile([P, short], F32, name="new_y_short")
-        nc.vector.tensor_tensor(new_y_short[:], new_ps[0][:, 0:short], y_short[:], MULT)
+        z_early = psum.tile([P, HALF], F32, name="z_early", tag="product0")
+        y_early = keep.tile([P, HALF], F32, name="y_early")
+        project_rows(z_early, y_early, 0, 0, HALF)
+        new_y_early = keep.tile([P, HALF], F32, name="new_y_early", tag="new_y_early")
+        nc.vector.tensor_tensor(new_y_early[:], new_ps[0][:], y_early[:], MULT)
 
         z_first = psum.tile([P, HALF], F32, name="z_first")
         y_first = keep.tile([P, HALF], F32, name="y_first", tag="y_first")
         project_rows(z_first, y_first, 1, 0, HALF)
         nc.vector.tensor_tensor(new_y[:, 0:HALF], new_ps[0][:], y_first[:], MULT)
-        nc.vector.tensor_tensor(summed[:, 0:short], new_y_short[:], old_mem0[:, 0:short], ADD)
+        nc.vector.tensor_tensor(summed[:, 0:HALF], new_y_early[:], old_mem0[:, 0:HALF], ADD)
         old_mem1 = keep.tile([P, S], F32, name="old_mem1", tag="y_first")
         nc.vector.tensor_tensor(old_mem1[:], window[1][:].indirect(slot_sb[:]), old_sb[:], MULT)
 
-        turned = {}
-        for n, (first, count) in list(enumerate(pieces))[1:]:
-            z = psum.tile([P, HALF], F32, name="z", tag="product%d" % n)
-            for at in range(first, first + count, P):
-                nc.tensor.matmul_mx(
-                    out=z[:, at - first : at - first + P],
-                    lhsT=x_codes[:, at : at + P].bitcast(FP4X4),
-                    lhsT_scale=x_bytes[:, at : at + P],
-                    rhs=w_codes[:, 0:P].bitcast(FP8X4),
-                    rhs_scale=w_scales[:, 0:P],
-                    start=True,
-                    stop=True,
-                )
-            y = keep.tile([P, count], F32, name="y%d" % n)
-            nc.scalar.activation(y[:], z[:, 0:count], TANH)
-            scaled = keep.tile([P, count], F32, name="scaled%d" % n)
-            for i in range(count // P):
-                col = first // P + i
-                nc.scalar.activation(scaled[:, i * P : (i + 1) * P], y[:, i * P : (i + 1) * P], COPY, scale=new_cols[:, col : col + 1])
-            turned[n] = psum.tile([P, HALF], F32, name="turned%d" % n)
-            for i in range(count // P):
-                nc.tensor.transpose(turned[n][:, i * P : (i + 1) * P], scaled[:, i * P : (i + 1) * P], ident[:])
+        z = psum.tile([P, HALF], F32, name="z", tag="product1")
+        for i in range(HALF // P):
+            at = HALF + i * P
+            nc.tensor.matmul_mx(
+                out=z[:, i * P : (i + 1) * P],
+                lhsT=x_codes[:, at : at + P].bitcast(FP4X4),
+                lhsT_scale=x_bytes[:, at : at + P],
+                rhs=w_codes[:, 0:P].bitcast(FP8X4),
+                rhs_scale=w_scales[:, 0:P],
+                start=True,
+                stop=True,
+            )
+        y = keep.tile([P, HALF], F32, name="y")
+        nc.scalar.activation(y[:], z[:], TANH)
+        scaled = keep.tile([P, HALF], F32, name="scaled")
+        turned = psum.tile([P, HALF], F32, name="turned")
+        for i in range(HALF // P):
+            col = HALF // P + i
+            nc.scalar.activation(scaled[:, i * P : (i + 1) * P], y[:, i * P : (i + 1) * P], COPY, scale=new_cols[:, col : col + 1])
+        for i in range(HALF // P):
+            nc.tensor.transpose(turned[:, i * P : (i + 1) * P], scaled[:, i * P : (i + 1) * P], ident[:])
 
-        def add(n):
-            first, count = pieces[n]
+        def add(first, count):
             cols = slice(first, first + count)
-            nc.vector.tensor_tensor(summed[:, cols], turned[n][:, 0:count], old_mem0[:, cols], ADD)
+            nc.vector.tensor_tensor(summed[:, cols], turned[:, first - HALF : first - HALF + count], old_mem0[:, cols], ADD)
 
-        def scatter(n):
-            first, count = pieces[n]
+        def scatter(first, count):
             nc.scalar.activation(window[0][:].indirect(entries(slot_sb, first, count)), summed[:, first : first + count], COPY)
 
         def put(first, count):
             cols = slice(first, first + count)
             nc.vector.tensor_tensor(window[1][:].indirect(entries(slot_sb, first, count)), old_mem1[:, cols], new_y[:, cols], ADD)
 
-        scatter(0)
-        z_second = psum.tile([P, HALF], F32, name="z_second", tag="new0")
-        y_second = keep.tile([P, HALF], F32, name="y_second")
+        short = S - 2 * PIECE
+        scatter(0, PIECE)
+        z_second = psum.tile([P, HALF], F32, name="z_second", tag="product2")
+        y_second = keep.tile([P, HALF], F32, name="y_second", tag="new_y_early")
         project_rows(z_second, y_second, 1, HALF, HALF)
-        add(1)
+        add(HALF, 2 * PIECE - HALF)
         put(0, short)
         nc.vector.tensor_tensor(new_y[:, HALF:S], new_ps[1][:], y_second[:], MULT)
-        add(2)
+        add(2 * PIECE, short)
         put(short, S - short)
-        scatter(1)
-        scatter(2)
+        scatter(PIECE, PIECE)
+        scatter(2 * PIECE, short)
         nc.sync.dma_start(out[0:P, :], window[0][:])
         nc.sync.dma_start(out[P:N, :], window[1][:])

@@ -88,17 +88,23 @@ def tile_picked_ema_tanh_p_kernel(tc, x_words, x_scales, mem, w1, old, new, offs
 
         old_sb = keep.tile([P, S], F32, name="old_sb")
         spread = [psum.tile([P, HALF], F32, name="spread", tag="product%d" % (1 + h)) for h in range(2)]
-        for h in range(2):
+        new_ps = [psum.tile([P, HALF], F32, name="new_ps%d" % h) for h in range(2)]
+
+        def spread_out(bank, cols, first):
             for i in range(HALF // P):
-                nc.tensor.transpose(spread[h][:, i * P : (i + 1) * P], old_cols[h][:, i : i + 1].to_broadcast([P, P]), ident[:])
+                nc.tensor.transpose(bank[:, i * P : (i + 1) * P], cols[:, first + i : first + i + 1].to_broadcast([P, P]), ident[:])
+
+        short = S - 2 * PIECE
+        spread_out(spread[0], old_cols[0], 0)
+        spread_out(new_ps[1], new_cols, HALF // P)
+        spread_out(spread[1], old_cols[1], 0)
+        spread_out(new_ps[0], new_cols, 0)
         nc.scalar.copy(old_sb[:, 0:HALF], spread[0][:])
+        new_sb = keep.tile([P, short], F32, name="new_sb")
+        nc.scalar.copy(new_sb[:], new_ps[1][:, HALF - short : HALF])
         w_bf = keep.tile([P, N, PACK], BF16, name="w_bf", tag="w_bf", align_bytes=64)
         nc.scalar.copy(w_bf[:].rearrange("p (c i) t -> p c t i", i=RUN), w_raw[:].rearrange("p t (c i) -> p c t i", i=RUN))
         nc.scalar.copy(old_sb[:, HALF:S], spread[1][:])
-        new_ps = [psum.tile([P, HALF], F32, name="new_ps", tag="new%d" % h) for h in range(2)]
-        for c in range(TILES):
-            at = c * P % HALF
-            nc.tensor.transpose(new_ps[c * P // HALF][:, at : at + P], new_cols[:, c : c + 1].to_broadcast([P, P]), ident[:])
 
         w_codes = keep.tile([P, N], U32, name="w_codes", align_bytes=64)
         w_scales = keep.tile([P, N], U8, name="w_scales", align_bytes=64)
@@ -106,12 +112,14 @@ def tile_picked_ema_tanh_p_kernel(tc, x_words, x_scales, mem, w1, old, new, offs
         nc.vector.tensor_copy(x_codes[:], words[:].indirect(offs_sb[:]))
         nc.vector.quantize_mx(out=w_codes[:].bitcast(FP8X4), scales=w_scales[:], in_=w_bf[:].rearrange("p n t -> p (n t)"))
 
-        gathered = keep.tile([P, S + HALF], F32, name="gathered", tag="w_raw", align_bytes=64)
+        early = S - short
+        fused = S - PIECE
+        gathered = keep.tile([P, S + PIECE], F32, name="gathered", tag="w_raw", align_bytes=64)
         old_mem0 = gathered[:, 0:S]
-        mem_late = gathered[:, S : S + HALF]
-        nc.vector.tensor_tensor(old_mem0[:, 0:HALF], window[0][:].indirect(entries(slot_sb, 0, HALF)), old_sb[:, 0:HALF], MULT)
-        nc.scalar.activation(mem_late, window[0][:].indirect(entries(slot_sb, HALF, HALF)), COPY)
-        nc.vector.tensor_tensor(old_mem0[:, HALF:S], mem_late, old_sb[:, HALF:S], MULT)
+        mem_late = gathered[:, S : S + PIECE]
+        nc.vector.tensor_tensor(old_mem0[:, 0:fused], window[0][:].indirect(entries(slot_sb, 0, fused)), old_sb[:, 0:fused], MULT)
+        nc.scalar.activation(mem_late, window[0][:].indirect(entries(slot_sb, fused, PIECE)), COPY)
+        nc.gpsimd.tensor_tensor(old_mem0[:, fused:S], mem_late, old_sb[:, fused:S], MULT)
 
         def project_rows(z, y, b, first, count):
             cols = slice(first, first + count)
@@ -125,24 +133,25 @@ def tile_picked_ema_tanh_p_kernel(tc, x_words, x_scales, mem, w1, old, new, offs
                 start=True,
                 stop=True,
             )
-            nc.scalar.activation(y[:], z[:, 0:count], TANH)
+            nc.scalar.activation(y, z[:, 0:count], TANH)
 
         summed = keep.tile([P, S], F32, name="summed")
         new_y = keep.tile([P, S], F32, name="new_y")
 
-        z_early = psum.tile([P, HALF], F32, name="z_early", tag="product0")
-        y_early = keep.tile([P, HALF], F32, name="y_early")
-        project_rows(z_early, y_early, 0, 0, HALF)
-        new_y_early = keep.tile([P, HALF], F32, name="new_y_early", tag="new_y_early")
-        nc.vector.tensor_tensor(new_y_early[:], new_ps[0][:], y_early[:], MULT)
-
-        z_first = psum.tile([P, HALF], F32, name="z_first")
-        y_first = keep.tile([P, HALF], F32, name="y_first", tag="y_first")
-        project_rows(z_first, y_first, 1, 0, HALF)
-        nc.vector.tensor_tensor(new_y[:, 0:HALF], new_ps[0][:], y_first[:], MULT)
-        nc.vector.tensor_tensor(summed[:, 0:HALF], new_y_early[:], old_mem0[:, 0:HALF], ADD)
-        old_mem1 = keep.tile([P, S], F32, name="old_mem1", tag="y_first")
+        y_early = keep.tile([P, HALF], F32, name="y_early", tag="y_early")
+        for n, tag in enumerate(("product0", "turned1")):
+            z_early = psum.tile([P, HALF], F32, name="z_early", tag=tag)
+            project_rows(z_early, y_early[:, n * short : (n + 1) * short], 0, n * short, short)
+        new_y_early = new_y[:, HALF:S]
+        nc.vector.tensor_tensor(new_y_early, new_ps[0][:], y_early[:], MULT)
+        nc.vector.tensor_tensor(summed[:, 0:HALF], new_y_early, old_mem0[:, 0:HALF], ADD)
+        old_mem1 = keep.tile([P, S], F32, name="old_mem1", tag="y_early")
         nc.vector.tensor_tensor(old_mem1[:], window[1][:].indirect(slot_sb[:]), old_sb[:], MULT)
+
+        y_rows = keep.tile([P, S], F32, name="y_rows")
+        for h in range(2):
+            z_rows = psum.tile([P, HALF], F32, name="z_rows", tag=("rows", "product2")[h])
+            project_rows(z_rows, y_rows[:, h * HALF : (h + 1) * HALF], 1, h * HALF, HALF)
 
         z = psum.tile([P, HALF], F32, name="z", tag="product1")
         for i in range(HALF // P):
@@ -158,17 +167,17 @@ def tile_picked_ema_tanh_p_kernel(tc, x_words, x_scales, mem, w1, old, new, offs
             )
         y = keep.tile([P, HALF], F32, name="y")
         nc.scalar.activation(y[:], z[:], TANH)
-        scaled = keep.tile([P, HALF], F32, name="scaled")
-        turned = psum.tile([P, HALF], F32, name="turned")
-        for i in range(HALF // P):
-            col = HALF // P + i
-            nc.scalar.activation(scaled[:, i * P : (i + 1) * P], y[:, i * P : (i + 1) * P], COPY, scale=new_cols[:, col : col + 1])
-        for i in range(HALF // P):
-            nc.tensor.transpose(turned[:, i * P : (i + 1) * P], scaled[:, i * P : (i + 1) * P], ident[:])
 
-        def add(first, count):
-            cols = slice(first, first + count)
-            nc.vector.tensor_tensor(summed[:, cols], turned[:, first - HALF : first - HALF + count], old_mem0[:, cols], ADD)
+        def turn(first, scaled, turned):
+            for at in range(0, short, P):
+                col = (first + at) // P
+                nc.scalar.activation(scaled[:, at : at + P], y[:, first - HALF + at : first - HALF + at + P], COPY, scale=new_cols[:, col : col + 1])
+            for at in range(0, short, P):
+                nc.tensor.transpose(turned[:, at : at + P], scaled[:, at : at + P], ident[:])
+
+        def add(first, turned):
+            cols = slice(first, first + short)
+            nc.vector.tensor_tensor(summed[:, cols], turned[:, 0:short], old_mem0[:, cols], ADD)
 
         def scatter(first, count):
             nc.scalar.activation(window[0][:].indirect(entries(slot_sb, first, count)), summed[:, first : first + count], COPY)
@@ -177,15 +186,17 @@ def tile_picked_ema_tanh_p_kernel(tc, x_words, x_scales, mem, w1, old, new, offs
             cols = slice(first, first + count)
             nc.vector.tensor_tensor(window[1][:].indirect(entries(slot_sb, first, count)), old_mem1[:, cols], new_y[:, cols], ADD)
 
-        short = S - 2 * PIECE
+        turned = [psum.tile([P, HALF], F32, name="turned", tag="turned%d" % n) for n in range(2)]
+        scaled = keep.tile([P, short], F32, name="scaled")
+        turn(HALF, scaled, turned[0])
         scatter(0, PIECE)
-        z_second = psum.tile([P, HALF], F32, name="z_second", tag="product2")
-        y_second = keep.tile([P, HALF], F32, name="y_second", tag="new_y_early")
-        project_rows(z_second, y_second, 1, HALF, HALF)
-        add(HALF, 2 * PIECE - HALF)
+        turn(early, old_mem0[:, 0:short], turned[1])
+        nc.gpsimd.tensor_tensor(new_y[:, early:S], new_sb[:], y_rows[:, early:S], MULT)
+        nc.vector.tensor_tensor(new_y[:, 0:HALF], new_ps[0][:], y_rows[:, 0:HALF], MULT)
+        add(HALF, turned[0])
+        nc.vector.tensor_tensor(new_y[:, HALF:early], new_ps[1][:, 0 : early - HALF], y_rows[:, HALF:early], MULT)
         put(0, short)
-        nc.vector.tensor_tensor(new_y[:, HALF:S], new_ps[1][:], y_second[:], MULT)
-        add(2 * PIECE, short)
+        add(early, turned[1])
         put(short, S - short)
         scatter(PIECE, PIECE)
         scatter(2 * PIECE, short)

@@ -29,6 +29,8 @@ SCALE_ROWS = K // 32
 QUADRANT = 32
 TOP = P - 16
 PIECE = 384
+FUSED = 640
+LEAD = 448
 RUN = 4
 
 
@@ -67,12 +69,14 @@ def tile_picked_ema_tanh_p_kernel(tc, x_words, x_scales, mem, w1, old, new, offs
         nc.sync.dma_start(window[0][:], mem[0:P, :])
         nc.sync.dma_start(slot_sb[:], slot)
 
-        picked = keep.tile([P, S], U8, name="picked", align_bytes=64)
+        picked = keep.tile([P, S], U8, name="picked", tag="picked", align_bytes=64)
         nc.vector.tensor_copy(picked[:], scales[:].indirect(offs_sb[:]))
         step = SCALE_ROWS // (P // QUADRANT)
         for r in range(step):
             nc.sync.dma_start(x_bytes[r:P:QUADRANT, :].bitcast(I32), picked[TOP + r : P : step, :].bitcast(I32))
         nc.sync.dma_start(window[1][:], mem[P : 2 * P, :])
+        new_late = keep.tile([P, S - LEAD], F32, name="new_late", tag="picked", align_bytes=64)
+        nc.sync.dma_start(new_late[:], new[:, LEAD:S])
 
         weight_ps = psum.tile([P, HALF], F32, name="weight_ps", tag="product0")
         nc.tensor.transpose(weight_ps[:, 0:P], weight_rows[:], ident[:])
@@ -88,7 +92,7 @@ def tile_picked_ema_tanh_p_kernel(tc, x_words, x_scales, mem, w1, old, new, offs
 
         old_sb = keep.tile([P, S], F32, name="old_sb")
         spread = [psum.tile([P, HALF], F32, name="spread", tag="product%d" % (1 + h)) for h in range(2)]
-        new_ps = [psum.tile([P, HALF], F32, name="new_ps%d" % h) for h in range(2)]
+        new_ps = psum.tile([P, HALF], F32, name="new_ps")
 
         def spread_out(bank, cols, first):
             for i in range(HALF // P):
@@ -96,12 +100,9 @@ def tile_picked_ema_tanh_p_kernel(tc, x_words, x_scales, mem, w1, old, new, offs
 
         short = S - 2 * PIECE
         spread_out(spread[0], old_cols[0], 0)
-        spread_out(new_ps[1], new_cols, HALF // P)
         spread_out(spread[1], old_cols[1], 0)
-        spread_out(new_ps[0], new_cols, 0)
+        spread_out(new_ps, new_cols, 0)
         nc.scalar.copy(old_sb[:, 0:HALF], spread[0][:])
-        new_sb = keep.tile([P, short], F32, name="new_sb")
-        nc.scalar.copy(new_sb[:], new_ps[1][:, HALF - short : HALF])
         w_bf = keep.tile([P, N, PACK], BF16, name="w_bf", tag="w_bf", align_bytes=64)
         nc.scalar.copy(w_bf[:].rearrange("p (c i) t -> p c t i", i=RUN), w_raw[:].rearrange("p t (c i) -> p c t i", i=RUN))
         nc.scalar.copy(old_sb[:, HALF:S], spread[1][:])
@@ -113,12 +114,12 @@ def tile_picked_ema_tanh_p_kernel(tc, x_words, x_scales, mem, w1, old, new, offs
         nc.vector.quantize_mx(out=w_codes[:].bitcast(FP8X4), scales=w_scales[:], in_=w_bf[:].rearrange("p n t -> p (n t)"))
 
         early = S - short
-        fused = S - PIECE
-        gathered = keep.tile([P, S + PIECE], F32, name="gathered", tag="w_raw", align_bytes=64)
+        fused = FUSED
+        gathered = keep.tile([P, 2 * S - fused], F32, name="gathered", tag="w_raw", align_bytes=64)
         old_mem0 = gathered[:, 0:S]
-        mem_late = gathered[:, S : S + PIECE]
+        mem_late = gathered[:, S : 2 * S - fused]
         nc.vector.tensor_tensor(old_mem0[:, 0:fused], window[0][:].indirect(entries(slot_sb, 0, fused)), old_sb[:, 0:fused], MULT)
-        nc.scalar.activation(mem_late, window[0][:].indirect(entries(slot_sb, fused, PIECE)), COPY)
+        nc.scalar.activation(mem_late, window[0][:].indirect(entries(slot_sb, fused, S - fused)), COPY)
         nc.gpsimd.tensor_tensor(old_mem0[:, fused:S], mem_late, old_sb[:, fused:S], MULT)
 
         def project_rows(z, y, b, first, count):
@@ -143,7 +144,7 @@ def tile_picked_ema_tanh_p_kernel(tc, x_words, x_scales, mem, w1, old, new, offs
             z_early = psum.tile([P, HALF], F32, name="z_early", tag=tag)
             project_rows(z_early, y_early[:, n * short : (n + 1) * short], 0, n * short, short)
         new_y_early = new_y[:, HALF:S]
-        nc.vector.tensor_tensor(new_y_early, new_ps[0][:], y_early[:], MULT)
+        nc.vector.tensor_tensor(new_y_early, new_ps[:], y_early[:], MULT)
         nc.vector.tensor_tensor(summed[:, 0:HALF], new_y_early, old_mem0[:, 0:HALF], ADD)
         old_mem1 = keep.tile([P, S], F32, name="old_mem1", tag="y_early")
         nc.vector.tensor_tensor(old_mem1[:], window[1][:].indirect(slot_sb[:]), old_sb[:], MULT)
@@ -154,7 +155,7 @@ def tile_picked_ema_tanh_p_kernel(tc, x_words, x_scales, mem, w1, old, new, offs
             project_rows(z_rows, y_rows[:, h * HALF : (h + 1) * HALF], 1, h * HALF, HALF)
 
         z = psum.tile([P, HALF], F32, name="z", tag="product1")
-        for i in range(HALF // P):
+        for i in range(short // P):
             at = HALF + i * P
             nc.tensor.matmul_mx(
                 out=z[:, i * P : (i + 1) * P],
@@ -165,8 +166,11 @@ def tile_picked_ema_tanh_p_kernel(tc, x_words, x_scales, mem, w1, old, new, offs
                 start=True,
                 stop=True,
             )
-        y = keep.tile([P, HALF], F32, name="y")
-        nc.scalar.activation(y[:], z[:], TANH)
+        y = keep.tile([P, short], F32, name="y")
+        nc.scalar.activation(y[:], z[:, 0:short], TANH)
+        z_last = psum.tile([P, HALF], F32, name="z_last")
+        y_last = keep.tile([P, short], F32, name="y_last")
+        project_rows(z_last, y_last[:], 0, early, short)
 
         def turn(first, scaled, turned):
             for at in range(0, short, P):
@@ -182,23 +186,23 @@ def tile_picked_ema_tanh_p_kernel(tc, x_words, x_scales, mem, w1, old, new, offs
         def scatter(first, count):
             nc.scalar.activation(window[0][:].indirect(entries(slot_sb, first, count)), summed[:, first : first + count], COPY)
 
-        def put(first, count):
-            cols = slice(first, first + count)
-            nc.vector.tensor_tensor(window[1][:].indirect(entries(slot_sb, first, count)), old_mem1[:, cols], new_y[:, cols], ADD)
-
-        turned = [psum.tile([P, HALF], F32, name="turned", tag="turned%d" % n) for n in range(2)]
+        turned = psum.tile([P, HALF], F32, name="turned", tag="turned0")
         scaled = keep.tile([P, short], F32, name="scaled")
-        turn(HALF, scaled, turned[0])
+        turn(HALF, scaled, turned)
         scatter(0, PIECE)
-        turn(early, old_mem0[:, 0:short], turned[1])
-        nc.gpsimd.tensor_tensor(new_y[:, early:S], new_sb[:], y_rows[:, early:S], MULT)
-        nc.vector.tensor_tensor(new_y[:, 0:HALF], new_ps[0][:], y_rows[:, 0:HALF], MULT)
-        add(HALF, turned[0])
-        nc.vector.tensor_tensor(new_y[:, HALF:early], new_ps[1][:, 0 : early - HALF], y_rows[:, HALF:early], MULT)
-        put(0, short)
-        add(early, turned[1])
-        put(short, S - short)
+        work = keep.tile([P, LEAD + short], F32, name="work")
+        middle = early - LEAD
+        summed1 = keep.tile([P, LEAD], F32, name="summed1")
+        nc.gpsimd.tensor_tensor(work[:, LEAD : LEAD + short], new_late[:, middle : S - LEAD], y_rows[:, early:S], MULT)
+        nc.vector.tensor_tensor(work[:, 0:LEAD], new_ps[:, 0:LEAD], y_rows[:, 0:LEAD], MULT)
+        add(HALF, turned)
+        nc.vector.tensor_tensor(summed1[:], work[:, 0:LEAD], old_mem1[:, 0:LEAD], ADD)
+        nc.vector.tensor_copy(window[1][:].indirect(entries(slot_sb, 0, LEAD)), summed1[:])
         scatter(PIECE, PIECE)
+        nc.gpsimd.tensor_tensor(work[:, LEAD - short : LEAD], new_late[:, middle : S - LEAD], y_last[:], MULT)
+        nc.gpsimd.tensor_tensor(summed[:, early:S], work[:, LEAD - short : LEAD], old_mem0[:, early:S], ADD)
+        nc.gpsimd.tensor_tensor(work[:, LEAD - middle : LEAD], new_late[:, 0:middle], y_rows[:, LEAD:early], MULT)
+        nc.vector.tensor_tensor(window[1][:].indirect(entries(slot_sb, LEAD, S - LEAD)), old_mem1[:, LEAD:S], work[:, LEAD - middle : LEAD + short], ADD)
         scatter(2 * PIECE, short)
         nc.sync.dma_start(out[0:P, :], window[0][:])
         nc.sync.dma_start(out[P:N, :], window[1][:])

@@ -30,7 +30,7 @@ QUADRANT = 32
 TOP = P - 16
 PIECE = 384
 FUSED = 640
-LEAD = 448
+LEAD = 256
 RUN = 4
 
 
@@ -137,25 +137,27 @@ def tile_picked_ema_tanh_p_kernel(tc, x_words, x_scales, mem, w1, old, new, offs
             nc.scalar.activation(y, z[:, 0:count], TANH)
 
         summed = keep.tile([P, S], F32, name="summed")
-        new_y = keep.tile([P, S], F32, name="new_y")
+        new_y = keep.tile([P, HALF], F32, name="new_y")
 
         y_early = keep.tile([P, HALF], F32, name="y_early", tag="y_early")
         for n, tag in enumerate(("product0", "turned1")):
             z_early = psum.tile([P, HALF], F32, name="z_early", tag=tag)
             project_rows(z_early, y_early[:, n * short : (n + 1) * short], 0, n * short, short)
-        new_y_early = new_y[:, HALF:S]
-        nc.vector.tensor_tensor(new_y_early, new_ps[:], y_early[:], MULT)
-        nc.vector.tensor_tensor(summed[:, 0:HALF], new_y_early, old_mem0[:, 0:HALF], ADD)
-        old_mem1 = keep.tile([P, S], F32, name="old_mem1", tag="y_early")
-        nc.vector.tensor_tensor(old_mem1[:], window[1][:].indirect(slot_sb[:]), old_sb[:], MULT)
-
         y_rows = keep.tile([P, S], F32, name="y_rows")
-        for h in range(2):
-            z_rows = psum.tile([P, HALF], F32, name="z_rows", tag=("rows", "product2")[h])
-            project_rows(z_rows, y_rows[:, h * HALF : (h + 1) * HALF], 1, h * HALF, HALF)
+        z_rows = psum.tile([P, HALF], F32, name="z_rows", tag="rows")
+        project_rows(z_rows, y_rows[:, 0:HALF], 1, 0, HALF)
+
+        work = keep.tile([P, S - LEAD], F32, name="work")
+        nc.vector.tensor_tensor(new_y[:], new_ps[:], y_early[:], MULT)
+        nc.vector.tensor_tensor(work[:, 0:LEAD], new_ps[:, 0:LEAD], y_rows[:, 0:LEAD], MULT)
+        nc.vector.tensor_tensor(summed[:, 0:HALF], new_y[:], old_mem0[:, 0:HALF], ADD)
+        old_mem1 = keep.tile([P, S], F32, name="old_mem1", tag="y_early")
+        for first, count in ((0, LEAD), (LEAD, S - LEAD)):
+            cols = slice(first, first + count)
+            nc.vector.tensor_tensor(old_mem1[:, cols], window[1][:].indirect(entries(slot_sb, first, count)), old_sb[:, cols], MULT)
 
         z = psum.tile([P, HALF], F32, name="z", tag="product1")
-        for i in range(short // P):
+        for i in range(HALF // P):
             at = HALF + i * P
             nc.tensor.matmul_mx(
                 out=z[:, i * P : (i + 1) * P],
@@ -166,11 +168,10 @@ def tile_picked_ema_tanh_p_kernel(tc, x_words, x_scales, mem, w1, old, new, offs
                 start=True,
                 stop=True,
             )
-        y = keep.tile([P, short], F32, name="y")
-        nc.scalar.activation(y[:], z[:, 0:short], TANH)
-        z_last = psum.tile([P, HALF], F32, name="z_last")
-        y_last = keep.tile([P, short], F32, name="y_last")
-        project_rows(z_last, y_last[:], 0, early, short)
+        y = keep.tile([P, HALF], F32, name="y")
+        nc.scalar.activation(y[:], z[:], TANH)
+        z_late = psum.tile([P, HALF], F32, name="z_late", tag="product2")
+        project_rows(z_late, y_rows[:, HALF:S], 1, HALF, HALF)
 
         def turn(first, scaled, turned):
             for at in range(0, short, P):
@@ -186,23 +187,20 @@ def tile_picked_ema_tanh_p_kernel(tc, x_words, x_scales, mem, w1, old, new, offs
         def scatter(first, count):
             nc.scalar.activation(window[0][:].indirect(entries(slot_sb, first, count)), summed[:, first : first + count], COPY)
 
-        turned = psum.tile([P, HALF], F32, name="turned", tag="turned0")
+        turned = [psum.tile([P, HALF], F32, name="turned", tag="turned%d" % n) for n in range(2)]
         scaled = keep.tile([P, short], F32, name="scaled")
-        turn(HALF, scaled, turned)
+        turn(HALF, scaled, turned[0])
         scatter(0, PIECE)
-        work = keep.tile([P, LEAD + short], F32, name="work")
-        middle = early - LEAD
+        turn(early, old_mem0[:, 0:short], turned[1])
         summed1 = keep.tile([P, LEAD], F32, name="summed1")
-        nc.gpsimd.tensor_tensor(work[:, LEAD : LEAD + short], new_late[:, middle : S - LEAD], y_rows[:, early:S], MULT)
-        nc.vector.tensor_tensor(work[:, 0:LEAD], new_ps[:, 0:LEAD], y_rows[:, 0:LEAD], MULT)
-        add(HALF, turned)
         nc.vector.tensor_tensor(summed1[:], work[:, 0:LEAD], old_mem1[:, 0:LEAD], ADD)
+        add(HALF, turned[0])
         nc.vector.tensor_copy(window[1][:].indirect(entries(slot_sb, 0, LEAD)), summed1[:])
         scatter(PIECE, PIECE)
-        nc.gpsimd.tensor_tensor(work[:, LEAD - short : LEAD], new_late[:, middle : S - LEAD], y_last[:], MULT)
-        nc.gpsimd.tensor_tensor(summed[:, early:S], work[:, LEAD - short : LEAD], old_mem0[:, early:S], ADD)
-        nc.gpsimd.tensor_tensor(work[:, LEAD - middle : LEAD], new_late[:, 0:middle], y_rows[:, LEAD:early], MULT)
-        nc.vector.tensor_tensor(window[1][:].indirect(entries(slot_sb, LEAD, S - LEAD)), old_mem1[:, LEAD:S], work[:, LEAD - middle : LEAD + short], ADD)
+        rest = work[:]
+        nc.gpsimd.tensor_tensor(rest, new_late[:], y_rows[:, LEAD:S], MULT)
+        add(early, turned[1])
+        nc.vector.tensor_tensor(window[1][:].indirect(entries(slot_sb, LEAD, S - LEAD)), old_mem1[:, LEAD:S], rest, ADD)
         scatter(2 * PIECE, short)
         nc.sync.dma_start(out[0:P, :], window[0][:])
         nc.sync.dma_start(out[P:N, :], window[1][:])

@@ -46,7 +46,7 @@ def tile_picked_ema_tanh_p_kernel(tc, x_words, x_scales, mem, w1, old, new, offs
 
         offs_sb = keep.tile([P, S // 16], U16, name="offs_sb")
         slot_sb = keep.tile([P, S // 16], U16, name="slot_sb")
-        words = keep.tile([P, 2 * T], U16, name="words", align_bytes=64)
+        words = keep.tile([P, T], U16, name="words", align_bytes=64)
         scales = keep.tile([P, T], U8, name="scales", tag="window1", align_bytes=64)
         w_raw = keep.tile([P, PACK, N], F32, name="w_raw", tag="w_raw", align_bytes=64)
         window = [keep.tile([P, U], F32, name="window%d" % b, tag="window%d" % b, align_bytes=64) for b in range(ROW_GROUPS)]
@@ -55,7 +55,6 @@ def tile_picked_ema_tanh_p_kernel(tc, x_words, x_scales, mem, w1, old, new, offs
         ident = keep.tile([P, P], F32, name="ident")
 
         nc.vector.memset(scales[0:TOP, :].bitcast(I32), 0)
-        nc.vector.memset(words[:].bitcast(I32)[:, T // 2 : T], 0)
         nc.gpsimd.memset(weight_rows[0:TOP, :], 0.0)
         make_identity(nc, ident[:])
         nc.gpsimd.memset(x_bytes[:].bitcast(I32), 0)
@@ -63,8 +62,8 @@ def tile_picked_ema_tanh_p_kernel(tc, x_words, x_scales, mem, w1, old, new, offs
         nc.sync.dma_start(offs_sb[:], offs)
         nc.sync.dma_start(weight_rows[TOP : TOP + TILES, :], new[0].rearrange("(c j) -> c j", j=P))
         nc.scalar.dma_start(scales[TOP:P, :].bitcast(I32), x_scales[0].bitcast(I32))
-        nc.sync.dma_start(words[:].bitcast(I32)[:, 0 : T // 2], x_words[0].bitcast(I32))
         nc.sync.dma_start(w_raw[:], w1.rearrange("(p t) n -> p t n", t=PACK))
+        nc.sync.dma_start(words[:].bitcast(I32), x_words[0].bitcast(I32))
         nc.scalar.dma_start(weight_rows[TOP + TILES : P, :], old[0].rearrange("(c j) -> c j", j=P))
         nc.sync.dma_start(window[0][:], mem[0:P, :])
         nc.sync.dma_start(slot_sb[:], slot)
@@ -102,20 +101,24 @@ def tile_picked_ema_tanh_p_kernel(tc, x_words, x_scales, mem, w1, old, new, offs
         spread_out(spread[0], old_cols[0], 0)
         spread_out(spread[1], old_cols[1], 0)
         spread_out(new_ps, new_cols, 0)
-        nc.scalar.copy(old_sb[:, 0:HALF], spread[0][:])
         w_bf = keep.tile([P, N, PACK], BF16, name="w_bf", tag="w_bf", align_bytes=64)
         nc.scalar.copy(w_bf[:].rearrange("p (c i) t -> p c t i", i=RUN), w_raw[:].rearrange("p t (c i) -> p c t i", i=RUN))
+        nc.scalar.copy(old_sb[:, 0:HALF], spread[0][:])
         nc.scalar.copy(old_sb[:, HALF:S], spread[1][:])
 
         w_codes = keep.tile([P, N], U32, name="w_codes", align_bytes=64)
         w_scales = keep.tile([P, N], U8, name="w_scales", align_bytes=64)
-        x_codes = keep.tile([P, S], U16, name="x_codes", align_bytes=64)
-        nc.vector.tensor_copy(x_codes[:], words[:].indirect(offs_sb[:]))
+        x_codes = [keep.tile([P, HALF], U16, name="x_codes", tag=("x_codes", "w_raw")[h], align_bytes=64) for h in range(2)]
+        nc.vector.tensor_copy(x_codes[0][:], words[:].indirect(entries(offs_sb, 0, HALF)))
         nc.vector.quantize_mx(out=w_codes[:].bitcast(FP8X4), scales=w_scales[:], in_=w_bf[:].rearrange("p n t -> p (n t)"))
+        nc.vector.tensor_copy(x_codes[1][:], words[:].indirect(entries(offs_sb, HALF, HALF)))
+
+        def codes(first, count):
+            return x_codes[first // HALF][:, first % HALF : first % HALF + count].bitcast(FP4X4)
 
         early = S - short
         fused = FUSED
-        gathered = keep.tile([P, 2 * S - fused], F32, name="gathered", tag="w_raw", align_bytes=64)
+        gathered = keep.tile([P, 2 * S - fused], F32, name="gathered", tag="w_bf", align_bytes=64)
         old_mem0 = gathered[:, 0:S]
         mem_late = gathered[:, S : 2 * S - fused]
         nc.vector.tensor_tensor(old_mem0[:, 0:fused], window[0][:].indirect(entries(slot_sb, 0, fused)), old_sb[:, 0:fused], MULT)
@@ -129,7 +132,7 @@ def tile_picked_ema_tanh_p_kernel(tc, x_words, x_scales, mem, w1, old, new, offs
                 out=z[:, 0:count],
                 lhsT=w_codes[:, rows].bitcast(FP8X4),
                 lhsT_scale=w_scales[:, rows],
-                rhs=x_codes[:, cols].bitcast(FP4X4),
+                rhs=codes(first, count),
                 rhs_scale=x_bytes[:, cols],
                 start=True,
                 stop=True,
@@ -161,7 +164,7 @@ def tile_picked_ema_tanh_p_kernel(tc, x_words, x_scales, mem, w1, old, new, offs
             at = HALF + i * P
             nc.tensor.matmul_mx(
                 out=z[:, i * P : (i + 1) * P],
-                lhsT=x_codes[:, at : at + P].bitcast(FP4X4),
+                lhsT=codes(at, P),
                 lhsT_scale=x_bytes[:, at : at + P],
                 rhs=w_codes[:, 0:P].bitcast(FP8X4),
                 rhs_scale=w_scales[:, 0:P],

@@ -65,8 +65,8 @@ def tile_picked_ema_tanh_p_kernel(tc, x_words, x_scales, mem, w1, old, new, offs
         nc.sync.dma_start(w_raw[:], w1.rearrange("(p t) n -> p t n", t=PACK))
         nc.sync.dma_start(words[:].bitcast(I32), x_words[0].bitcast(I32))
         nc.scalar.dma_start(weight_rows[TOP + TILES : P, :], old[0].rearrange("(c j) -> c j", j=P))
-        nc.sync.dma_start(window[0][:], mem[0:P, :])
         nc.sync.dma_start(slot_sb[:], slot)
+        nc.sync.dma_start(window[0][:], mem[0:P, :])
 
         picked = keep.tile([P, S], U8, name="picked", tag="picked", align_bytes=64)
         nc.vector.tensor_copy(picked[:], scales[:].indirect(offs_sb[:]))
@@ -205,5 +205,5 @@ def tile_picked_ema_tanh_p_kernel(tc, x_words, x_scales, mem, w1, old, new, offs
         add(early, turned[1])
         nc.vector.tensor_tensor(window[1][:].indirect(entries(slot_sb, LEAD, S - LEAD)), old_mem1[:, LEAD:S], rest, ADD)
         scatter(2 * PIECE, short)
-        nc.sync.dma_start(out[0:P, :], window[0][:])
+        nc.scalar.dma_start(out[0:P, :], window[0][:])
         nc.sync.dma_start(out[P:N, :], window[1][:])

@@ -51,7 +51,7 @@ def tile_picked_ema_tanh_p_kernel(tc, x_words, x_scales, mem, w1, old, new, offs
         w_raw = keep.tile([P, PACK, N], F32, name="w_raw", tag="w_raw", align_bytes=64)
         window = [keep.tile([P, U], F32, name="window%d" % b, tag="window%d" % b, align_bytes=64) for b in range(ROW_GROUPS)]
         x_bytes = keep.tile([P, S], U8, name="x_bytes", align_bytes=64)
-        weight_rows = keep.tile([P, P], F32, name="weight_rows")
+        weight_rows = keep.tile([P, P], F32, name="weight_rows", tag="w_bf", align_bytes=64)
         ident = keep.tile([P, P], F32, name="ident")
 
         nc.vector.memset(scales[0:TOP, :].bitcast(I32), 0)
@@ -80,7 +80,7 @@ def tile_picked_ema_tanh_p_kernel(tc, x_words, x_scales, mem, w1, old, new, offs
         weight_ps = psum.tile([P, HALF], F32, name="weight_ps", tag="product0")
         nc.tensor.transpose(weight_ps[:, 0:P], weight_rows[:], ident[:])
         old_cols = [
-            keep.tile([P, HALF // P], F32, name="old_first", tag="w_bf", align_bytes=64),
+            keep.tile([P, HALF // P], F32, name="old_first"),
             keep.tile([P, HALF // P], F32, name="old_second"),
         ]
         for h in range(2):

@@ -29,7 +29,7 @@ SCALE_ROWS = K // 32
 QUADRANT = 32
 TOP = P - 16
 PIECE = 384
-FUSED = 640
+FUSED = 672
 LEAD = 256
 RUN = 4
 

@@ -62,8 +62,8 @@ def tile_picked_ema_tanh_p_kernel(tc, x_words, x_scales, mem, w1, old, new, offs
         nc.sync.dma_start(offs_sb[:], offs)
         nc.sync.dma_start(weight_rows[TOP : TOP + TILES, :], new[0].rearrange("(c j) -> c j", j=P))
         nc.scalar.dma_start(scales[TOP:P, :].bitcast(I32), x_scales[0].bitcast(I32))
-        nc.sync.dma_start(w_raw[:], w1.rearrange("(p t) n -> p t n", t=PACK))
         nc.sync.dma_start(words[:].bitcast(I32), x_words[0].bitcast(I32))
+        nc.sync.dma_start(w_raw[:], w1.rearrange("(p t) n -> p t n", t=PACK))
         nc.scalar.dma_start(weight_rows[TOP + TILES : P, :], old[0].rearrange("(c j) -> c j", j=P))
         nc.sync.dma_start(slot_sb[:], slot)
         nc.sync.dma_start(window[0][:], mem[0:P, :])
@@ -108,15 +108,19 @@ def tile_picked_ema_tanh_p_kernel(tc, x_words, x_scales, mem, w1, old, new, offs
 
         w_codes = keep.tile([P, N], U32, name="w_codes", align_bytes=64)
         w_scales = keep.tile([P, N], U8, name="w_scales", align_bytes=64)
-        x_codes = [keep.tile([P, HALF], U16, name="x_codes", tag=("x_codes", "w_raw")[h], align_bytes=64) for h in range(2)]
-        nc.vector.tensor_copy(x_codes[0][:], words[:].indirect(entries(offs_sb, 0, HALF)))
+        early = S - short
+        x_codes = keep.tile([P, early], U16, name="x_codes", align_bytes=64)
+        x_last = keep.tile([P, short], U16, name="x_last", tag="w_raw", align_bytes=64)
+        nc.vector.tensor_copy(x_codes[:, 0:HALF], words[:].indirect(entries(offs_sb, 0, HALF)))
+        nc.vector.tensor_copy(x_codes[:, HALF:early], words[:].indirect(entries(offs_sb, HALF, short)))
         nc.vector.quantize_mx(out=w_codes[:].bitcast(FP8X4), scales=w_scales[:], in_=w_bf[:].rearrange("p n t -> p (n t)"))
-        nc.vector.tensor_copy(x_codes[1][:], words[:].indirect(entries(offs_sb, HALF, HALF)))
+        nc.vector.tensor_copy(x_last[:], words[:].indirect(entries(offs_sb, early, short)))
 
         def codes(first, count):
-            return x_codes[first // HALF][:, first % HALF : first % HALF + count].bitcast(FP4X4)
+            if first >= early:
+                return x_last[:, first - early : first - early + count].bitcast(FP4X4)
+            return x_codes[:, first : first + count].bitcast(FP4X4)
 
-        early = S - short
         fused = FUSED
         gathered = keep.tile([P, 2 * S - fused], F32, name="gathered", tag="w_bf", align_bytes=64)
         old_mem0 = gathered[:, 0:S]
@@ -126,17 +130,18 @@ def tile_picked_ema_tanh_p_kernel(tc, x_words, x_scales, mem, w1, old, new, offs
         nc.gpsimd.tensor_tensor(old_mem0[:, fused:S], mem_late, old_sb[:, fused:S], MULT)
 
         def project_rows(z, y, b, first, count):
-            cols = slice(first, first + count)
             rows = slice(b * P, (b + 1) * P)
-            nc.tensor.matmul_mx(
-                out=z[:, 0:count],
-                lhsT=w_codes[:, rows].bitcast(FP8X4),
-                lhsT_scale=w_scales[:, rows],
-                rhs=codes(first, count),
-                rhs_scale=x_bytes[:, cols],
-                start=True,
-                stop=True,
-            )
+            width = short if first + count > early else count
+            for at in range(0, count, width):
+                nc.tensor.matmul_mx(
+                    out=z[:, at : at + width],
+                    lhsT=w_codes[:, rows].bitcast(FP8X4),
+                    lhsT_scale=w_scales[:, rows],
+                    rhs=codes(first + at, width),
+                    rhs_scale=x_bytes[:, first + at : first + at + width],
+                    start=True,
+                    stop=True,
+                )
             nc.scalar.activation(y, z[:, 0:count], TANH)
 
         summed = keep.tile([P, S], F32, name="summed")

@@ -60,9 +60,9 @@ def tile_picked_ema_tanh_p_kernel(tc, x_words, x_scales, mem, w1, old, new, offs
         nc.gpsimd.memset(x_bytes[:].bitcast(I32), 0)
 
         nc.sync.dma_start(offs_sb[:], offs)
-        nc.sync.dma_start(weight_rows[TOP : TOP + TILES, :], new[0].rearrange("(c j) -> c j", j=P))
         nc.scalar.dma_start(scales[TOP:P, :].bitcast(I32), x_scales[0].bitcast(I32))
         nc.sync.dma_start(words[:].bitcast(I32), x_words[0].bitcast(I32))
+        nc.sync.dma_start(weight_rows[TOP : TOP + TILES, :], new[0].rearrange("(c j) -> c j", j=P))
         nc.sync.dma_start(w_raw[:], w1.rearrange("(p t) n -> p t n", t=PACK))
         nc.scalar.dma_start(weight_rows[TOP + TILES : P, :], old[0].rearrange("(c j) -> c j", j=P))
         nc.sync.dma_start(slot_sb[:], slot)

@@ -42,13 +42,14 @@ def tile_picked_ema_tanh_p_kernel(tc, x_words, x_scales, mem, w1, old, new, offs
     nc = tc.nc
     with ExitStack() as ctx:
         keep = ctx.enter_context(tc.tile_pool(name="keep", bufs=1))
+        shared = ctx.enter_context(tc.tile_pool(name="shared", bufs=1))
         psum = ctx.enter_context(tc.psum_pool(name="psum", bufs=1))
 
         offs_sb = keep.tile([P, S // 16], U16, name="offs_sb")
         slot_sb = keep.tile([P, S // 16], U16, name="slot_sb")
         words = keep.tile([P, T], U16, name="words", align_bytes=64)
         scales = keep.tile([P, T], U8, name="scales", tag="window1", align_bytes=64)
-        w_raw = keep.tile([P, PACK, N], F32, name="w_raw", tag="w_raw", align_bytes=64)
+        w_raw = shared.tile([P, PACK, N], F32, name="w_raw", offset=0, align_bytes=64)
         window = [keep.tile([P, U], F32, name="window%d" % b, tag="window%d" % b, align_bytes=64) for b in range(ROW_GROUPS)]
         x_bytes = keep.tile([P, S], U8, name="x_bytes", align_bytes=64)
         weight_rows = keep.tile([P, P], F32, name="weight_rows", tag="w_bf", align_bytes=64)
@@ -102,7 +103,9 @@ def tile_picked_ema_tanh_p_kernel(tc, x_words, x_scales, mem, w1, old, new, offs
         spread_out(spread[1], old_cols[1], 0)
         spread_out(new_ps, new_cols, 0)
         w_bf = keep.tile([P, N, PACK], BF16, name="w_bf", tag="w_bf", align_bytes=64)
-        nc.scalar.copy(w_bf[:].rearrange("p (c i) t -> p c t i", i=RUN), w_raw[:].rearrange("p t (c i) -> p c t i", i=RUN))
+        for b in range(ROW_GROUPS):
+            rows = slice(b * P, (b + 1) * P)
+            nc.scalar.copy(w_bf[:, rows, :].rearrange("p (c i) t -> p c t i", i=RUN), w_raw[:, :, rows].rearrange("p t (c i) -> p c t i", i=RUN))
         nc.scalar.copy(old_sb[:, 0:HALF], spread[0][:])
         nc.scalar.copy(old_sb[:, HALF:S], spread[1][:])
 
@@ -110,11 +113,17 @@ def tile_picked_ema_tanh_p_kernel(tc, x_words, x_scales, mem, w1, old, new, offs
         w_scales = keep.tile([P, N], U8, name="w_scales", align_bytes=64)
         early = S - short
         x_codes = keep.tile([P, early], U16, name="x_codes", align_bytes=64)
-        x_last = keep.tile([P, short], U16, name="x_last", tag="w_raw", align_bytes=64)
+        x_last = shared.tile([P, short], U16, name="x_last", offset=0, align_bytes=64)
         nc.vector.tensor_copy(x_codes[:, 0:HALF], words[:].indirect(entries(offs_sb, 0, HALF)))
         nc.vector.tensor_copy(x_codes[:, HALF:early], words[:].indirect(entries(offs_sb, HALF, short)))
-        nc.vector.quantize_mx(out=w_codes[:].bitcast(FP8X4), scales=w_scales[:], in_=w_bf[:].rearrange("p n t -> p (n t)"))
+
+        def quantise(b):
+            rows = slice(b * P, (b + 1) * P)
+            nc.vector.quantize_mx(out=w_codes[:, rows].bitcast(FP8X4), scales=w_scales[:, rows], in_=w_bf[:, rows, :].rearrange("p n t -> p (n t)"))
+
+        quantise(0)
         nc.vector.tensor_copy(x_last[:], words[:].indirect(entries(offs_sb, early, short)))
+        quantise(1)
 
         def codes(first, count):
             if first >= early:
@@ -122,7 +131,7 @@ def tile_picked_ema_tanh_p_kernel(tc, x_words, x_scales, mem, w1, old, new, offs
             return x_codes[:, first : first + count].bitcast(FP4X4)
 
         fused = FUSED
-        gathered = keep.tile([P, 2 * S - fused], F32, name="gathered", tag="w_bf", align_bytes=64)
+        gathered = shared.tile([P, 2 * S - fused], F32, name="gathered", offset=2 * short, align_bytes=64)
         old_mem0 = gathered[:, 0:S]
         mem_late = gathered[:, S : 2 * S - fused]
         nc.vector.tensor_tensor(old_mem0[:, 0:fused], window[0][:].indirect(entries(slot_sb, 0, fused)), old_sb[:, 0:fused], MULT)

from contextlib import ExitStack

import concourse.mybir as mybir
from concourse.masks import make_identity

K, T, S, N, U = 512, 2048, 1024, 256, 2048
P = 128
PACK = 4
FLOPS = 2 * K * S * N
BYTES = P * 2 * T + 16 * T + 4 * (2 * N * U + K * N + 2 * S) + 2 * 2 * P * (S // 16)

F32 = mybir.dt.float32
BF16 = mybir.dt.bfloat16
I32 = mybir.dt.int32
U32 = mybir.dt.uint32
U16 = mybir.dt.uint16
U8 = mybir.dt.uint8
FP8X4 = mybir.dt.float8_e4m3fn_x4
FP4X4 = mybir.dt.float4_e2m1fn_x4
MULT = mybir.AluOpType.mult
ADD = mybir.AluOpType.add
TANH = mybir.ActivationFunctionType.Tanh
COPY = mybir.ActivationFunctionType.Copy

ROW_GROUPS = N // P
TILES = S // P
HALF = 512
SCALE_ROWS = K // 32
QUADRANT = 32
TOP = P - 16
PIECE = 384
FUSED = 672
LEAD = 256
RUN = 4


def entries(lst, first, count):
    return lst[:, first // 16 : (first + count) // 16]


def tile_picked_ema_tanh_p_kernel(tc, x_words, x_scales, mem, w1, old, new, offs, slot, out):
    nc = tc.nc
    with ExitStack() as ctx:
        keep = ctx.enter_context(tc.tile_pool(name="keep", bufs=1))
        shared = ctx.enter_context(tc.tile_pool(name="shared", bufs=1))
        psum = ctx.enter_context(tc.psum_pool(name="psum", bufs=1))

        offs_sb = keep.tile([P, S // 16], U16, name="offs_sb")
        slot_sb = keep.tile([P, S // 16], U16, name="slot_sb")
        words = keep.tile([P, T], U16, name="words", align_bytes=64)
        scales = keep.tile([P, T], U8, name="scales", tag="window1", align_bytes=64)
        w_raw = shared.tile([P, PACK, N], F32, name="w_raw", offset=0, align_bytes=64)
        window = [keep.tile([P, U], F32, name="window%d" % b, tag="window%d" % b, align_bytes=64) for b in range(ROW_GROUPS)]
        x_bytes = keep.tile([P, S], U8, name="x_bytes", align_bytes=64)
        weight_rows = keep.tile([P, P], F32, name="weight_rows", tag="w_bf", align_bytes=64)
        ident = keep.tile([P, P], F32, name="ident")

        nc.vector.memset(scales[0:TOP, :].bitcast(I32), 0)
        nc.gpsimd.memset(weight_rows[0:TOP, :], 0.0)
        make_identity(nc, ident[:])
        nc.gpsimd.memset(x_bytes[:].bitcast(I32), 0)

        nc.sync.dma_start(offs_sb[:], offs)
        nc.scalar.dma_start(scales[TOP:P, :].bitcast(I32), x_scales[0].bitcast(I32))
        nc.sync.dma_start(words[:].bitcast(I32), x_words[0].bitcast(I32))
        nc.sync.dma_start(weight_rows[TOP : TOP + TILES, :], new[0].rearrange("(c j) -> c j", j=P))
        nc.sync.dma_start(w_raw[:], w1.rearrange("(p t) n -> p t n", t=PACK))
        nc.scalar.dma_start(weight_rows[TOP + TILES : P, :], old[0].rearrange("(c j) -> c j", j=P))
        nc.sync.dma_start(slot_sb[:], slot)
        nc.sync.dma_start(window[0][:], mem[0:P, :])

        picked = keep.tile([P, S], U8, name="picked", tag="picked", align_bytes=64)
        nc.vector.tensor_copy(picked[:], scales[:].indirect(offs_sb[:]))
        step = SCALE_ROWS // (P // QUADRANT)
        for r in range(step):
            nc.sync.dma_start(x_bytes[r:P:QUADRANT, :].bitcast(I32), picked[TOP + r : P : step, :].bitcast(I32))
        nc.sync.dma_start(window[1][:], mem[P : 2 * P, :])
        new_late = keep.tile([P, S - LEAD], F32, name="new_late", tag="picked", align_bytes=64)
        nc.sync.dma_start(new_late[:], new[:, LEAD:S])

        weight_ps = psum.tile([P, HALF], F32, name="weight_ps", tag="product0")
        nc.tensor.transpose(weight_ps[:, 0:P], weight_rows[:], ident[:])
        old_cols = [
            keep.tile([P, HALF // P], F32, name="old_first"),
            keep.tile([P, HALF // P], F32, name="old_second"),
        ]
        for h in range(2):
            at = TOP + TILES + h * HALF // P
            nc.scalar.copy(old_cols[h][:], weight_ps[:, at : at + HALF // P])
        new_cols = keep.tile([P, TILES], F32, name="new_cols")
        nc.scalar.copy(new_cols[:], weight_ps[:, TOP : TOP + TILES])

        old_sb = keep.tile([P, S], F32, name="old_sb")
        spread = [psum.tile([P, HALF], F32, name="spread", tag="product%d" % (1 + h)) for h in range(2)]
        new_ps = psum.tile([P, HALF], F32, name="new_ps")

        def spread_out(bank, cols, first):
            for i in range(HALF // P):
                nc.tensor.transpose(bank[:, i * P : (i + 1) * P], cols[:, first + i : first + i + 1].to_broadcast([P, P]), ident[:])

        short = S - 2 * PIECE
        spread_out(spread[0], old_cols[0], 0)
        spread_out(spread[1], old_cols[1], 0)
        spread_out(new_ps, new_cols, 0)
        w_bf = keep.tile([P, N, PACK], BF16, name="w_bf", tag="w_bf", align_bytes=64)
        for b in range(ROW_GROUPS):
            rows = slice(b * P, (b + 1) * P)
            nc.scalar.copy(w_bf[:, rows, :].rearrange("p (c i) t -> p c t i", i=RUN), w_raw[:, :, rows].rearrange("p t (c i) -> p c t i", i=RUN))
        nc.scalar.copy(old_sb[:, 0:HALF], spread[0][:])
        nc.scalar.copy(old_sb[:, HALF:S], spread[1][:])

        w_codes = keep.tile([P, N], U32, name="w_codes", align_bytes=64)
        w_scales = keep.tile([P, N], U8, name="w_scales", align_bytes=64)
        early = S - short
        x_codes = keep.tile([P, early], U16, name="x_codes", align_bytes=64)
        x_last = shared.tile([P, short], U16, name="x_last", offset=0, align_bytes=64)
        nc.vector.tensor_copy(x_codes[:, 0:HALF], words[:].indirect(entries(offs_sb, 0, HALF)))
        nc.vector.tensor_copy(x_codes[:, HALF:early], words[:].indirect(entries(offs_sb, HALF, short)))

        def quantise(b):
            rows = slice(b * P, (b + 1) * P)
            nc.vector.quantize_mx(out=w_codes[:, rows].bitcast(FP8X4), scales=w_scales[:, rows], in_=w_bf[:, rows, :].rearrange("p n t -> p (n t)"))

        quantise(0)
        nc.vector.tensor_copy(x_last[:], words[:].indirect(entries(offs_sb, early, short)))
        quantise(1)

        def codes(first, count):
            if first >= early:
                return x_last[:, first - early : first - early + count].bitcast(FP4X4)
            return x_codes[:, first : first + count].bitcast(FP4X4)

        fused = FUSED
        gathered = shared.tile([P, 2 * S - fused], F32, name="gathered", offset=2 * short, align_bytes=64)
        old_mem0 = gathered[:, 0:S]
        mem_late = gathered[:, S : 2 * S - fused]
        nc.vector.tensor_tensor(old_mem0[:, 0:fused], window[0][:].indirect(entries(slot_sb, 0, fused)), old_sb[:, 0:fused], MULT)
        nc.scalar.activation(mem_late, window[0][:].indirect(entries(slot_sb, fused, S - fused)), COPY)
        nc.gpsimd.tensor_tensor(old_mem0[:, fused:S], mem_late, old_sb[:, fused:S], MULT)

        def project_rows(z, y, b, first, count):
            rows = slice(b * P, (b + 1) * P)
            width = short if first + count > early else count
            for at in range(0, count, width):
                nc.tensor.matmul_mx(
                    out=z[:, at : at + width],
                    lhsT=w_codes[:, rows].bitcast(FP8X4),
                    lhsT_scale=w_scales[:, rows],
                    rhs=codes(first + at, width),
                    rhs_scale=x_bytes[:, first + at : first + at + width],
                    start=True,
                    stop=True,
                )
            nc.scalar.activation(y, z[:, 0:count], TANH)

        summed = keep.tile([P, S], F32, name="summed")
        new_y = keep.tile([P, HALF], F32, name="new_y")

        y_early = keep.tile([P, HALF], F32, name="y_early", tag="y_early")
        for n, tag in enumerate(("product0", "turned1")):
            z_early = psum.tile([P, HALF], F32, name="z_early", tag=tag)
            project_rows(z_early, y_early[:, n * short : (n + 1) * short], 0, n * short, short)
        y_rows = keep.tile([P, S], F32, name="y_rows")
        z_rows = psum.tile([P, HALF], F32, name="z_rows", tag="rows")
        project_rows(z_rows, y_rows[:, 0:HALF], 1, 0, HALF)

        work = keep.tile([P, S - LEAD], F32, name="work")
        nc.vector.tensor_tensor(new_y[:], new_ps[:], y_early[:], MULT)
        nc.vector.tensor_tensor(work[:, 0:LEAD], new_ps[:, 0:LEAD], y_rows[:, 0:LEAD], MULT)
        nc.vector.tensor_tensor(summed[:, 0:HALF], new_y[:], old_mem0[:, 0:HALF], ADD)
        old_mem1 = keep.tile([P, S], F32, name="old_mem1", tag="y_early")
        for first, count in ((0, LEAD), (LEAD, S - LEAD)):
            cols = slice(first, first + count)
            nc.vector.tensor_tensor(old_mem1[:, cols], window[1][:].indirect(entries(slot_sb, first, count)), old_sb[:, cols], MULT)

        z = psum.tile([P, HALF], F32, name="z", tag="product1")
        for i in range(HALF // P):
            at = HALF + i * P
            nc.tensor.matmul_mx(
                out=z[:, i * P : (i + 1) * P],
                lhsT=codes(at, P),
                lhsT_scale=x_bytes[:, at : at + P],
                rhs=w_codes[:, 0:P].bitcast(FP8X4),
                rhs_scale=w_scales[:, 0:P],
                start=True,
                stop=True,
            )
        y = keep.tile([P, HALF], F32, name="y")
        nc.scalar.activation(y[:], z[:], TANH)
        z_late = psum.tile([P, HALF], F32, name="z_late", tag="product2")
        project_rows(z_late, y_rows[:, HALF:S], 1, HALF, HALF)

        def turn(first, scaled, turned):
            for at in range(0, short, P):
                col = (first + at) // P
                nc.scalar.activation(scaled[:, at : at + P], y[:, first - HALF + at : first - HALF + at + P], COPY, scale=new_cols[:, col : col + 1])
            for at in range(0, short, P):
                nc.tensor.transpose(turned[:, at : at + P], scaled[:, at : at + P], ident[:])

        def add(first, turned):
            cols = slice(first, first + short)
            nc.vector.tensor_tensor(summed[:, cols], turned[:, 0:short], old_mem0[:, cols], ADD)

        def scatter(first, count):
            nc.scalar.activation(window[0][:].indirect(entries(slot_sb, first, count)), summed[:, first : first + count], COPY)

        turned = [psum.tile([P, HALF], F32, name="turned", tag="turned%d" % n) for n in range(2)]
        scaled = keep.tile([P, short], F32, name="scaled")
        turn(HALF, scaled, turned[0])
        scatter(0, PIECE)
        turn(early, old_mem0[:, 0:short], turned[1])
        summed1 = keep.tile([P, LEAD], F32, name="summed1")
        nc.vector.tensor_tensor(summed1[:], work[:, 0:LEAD], old_mem1[:, 0:LEAD], ADD)
        add(HALF, turned[0])
        nc.vector.tensor_copy(window[1][:].indirect(entries(slot_sb, 0, LEAD)), summed1[:])
        scatter(PIECE, PIECE)
        rest = work[:]
        nc.gpsimd.tensor_tensor(rest, new_late[:], y_rows[:, LEAD:S], MULT)
        add(early, turned[1])
        nc.vector.tensor_tensor(window[1][:].indirect(entries(slot_sb, LEAD, S - LEAD)), old_mem1[:, LEAD:S], rest, ADD)
        scatter(2 * PIECE, short)
        nc.scalar.dma_start(out[0:P, :], window[0][:])
        nc.sync.dma_start(out[P:N, :], window[1][:])
